import numpy as np
import ml_dtypes


def mxq(x, axis, fmt="e4m3"):
    dtype, down = {"e4m3": (ml_dtypes.float8_e4m3fn, 7), "e5m2": (ml_dtypes.float8_e5m2, 14)}[fmt]
    v = np.moveaxis(np.asarray(x, np.float32).astype(ml_dtypes.bfloat16).astype(np.float64), axis, -1)
    blocks = v.reshape(v.shape[:-1] + (-1, 32))
    amax = np.abs(blocks).max(-1, keepdims=True)
    byte = np.maximum(np.where(amax > 0, np.frexp(amax)[1] - 1 + 127, 0) - down, 1)
    scale = np.exp2(byte - 127.0)
    codes = (blocks / scale).astype(np.float32).astype(dtype).astype(np.float64)
    return np.moveaxis((codes * scale).reshape(v.shape), -1, axis)


WIDE = False


def mx_kscale(k):
    if not WIDE:
        return np.ones(k)
    levels = np.array([10, -10, 5, -5, 0])
    if k % 512:
        return np.exp2(np.random.permutation(np.resize(levels, k // 32))).repeat(32)
    a = np.empty((k // 512, 16))
    for p in range(k // 512):
        a[p, :8] = np.random.permutation(np.resize(levels, 8))
        for g in range(8):
            far = levels[np.abs(levels - a[p, g]) >= 10]
            a[p, g + 8] = far[np.random.randint(len(far))]
    return np.exp2(a.ravel()).repeat(32)


def f64(x):
    return np.asarray(x).astype(np.float64)


def striped(idx):
    return np.tile(idx.reshape(-1, 16).T, (8, 1)).astype(np.uint16)


def unstriped(offs):
    return offs[:16].T.reshape(-1).astype(np.int64)


K, T, S, N, U = 1024, 1024, 512, 256, 1024


def setup_inputs():
    n = np.random.standard_normal
    s = mx_kscale(K)[:, None]
    return {
        "xT": (n((K, T)) * s).astype(np.float32),
        "mem": n((N, U)).astype(np.float32),
        "w1": (n((K, N)) / np.sqrt(K) / s).astype(np.float32),
        "offs": striped(np.random.permutation(T)[:S]),
        "slot": striped(np.random.permutation(U)[:S]),
    }


def reference(xT, mem, w1, offs, slot):
    xq = mxq(f64(xT)[:, unstriped(offs)], 0, "e4m3")
    y = mxq(f64(w1), 0, "e4m3").T @ xq
    out = f64(mem).copy()
    out[:, unstriped(slot)] = f64(mem)[:, unstriped(slot)] + y
    return out

@@ -1,0 +1,156 @@
+from contextlib import ExitStack
+
+import concourse.mybir as mybir
+from concourse.masks import make_identity
+
+K, T, S, N, U = 1024, 1024, 512, 256, 1024
+FLOPS = 2 * K * N * S
+
+F32 = mybir.dt.float32
+BF16 = mybir.dt.bfloat16
+U32 = mybir.dt.uint32
+U16 = mybir.dt.uint16
+U8 = mybir.dt.uint8
+FP8X4 = mybir.dt.float8_e4m3fn_x4
+ADD = mybir.AluOpType.add
+
+P = 128
+
+
+def tile_picked_idxput_add_e_kernel(tc, xT, mem, w1, offs, slot, out):
+    nc = tc.nc
+    with ExitStack() as ctx:
+        keep = ctx.enter_context(tc.tile_pool(name="keep", bufs=1))
+        psum = ctx.enter_context(tc.psum_pool(name="psum", bufs=1))
+
+        x_pairs = xT.rearrange("(z p u e) t -> z u p e t", z=2, p=P, u=2, e=2)
+        w_rows = w1.rearrange("(z p j) m -> z p j m", z=2, p=P, j=4)
+
+        offs_sb = keep.tile([P, S // 16], U16, name="offs_sb")
+        slot_sb = keep.tile([P, S // 16], U16, name="slot_sb")
+
+        raw = [[keep.tile([P, 2, T // 2], F32, name="raw%d_%d" % (i, h)) for h in range(2)] for i in range(4)]
+        w_raw = [keep.tile([P, 4, N], F32, name="w_raw%d" % z) for z in range(2)]
+        store = [keep.tile([P, U], F32, name="store%d" % b) for b in range(2)]
+
+        def load_x(i, h):
+            nc.sync.dma_start(out=raw[i][h][:], in_=x_pairs[i // 2, i % 2][:, :, h * 512 : (h + 1) * 512])
+
+        load_x(0, 0)
+        load_x(0, 1)
+        nc.sync.dma_start(offs_sb[:], offs)
+        load_x(1, 0)
+        load_x(1, 1)
+        nc.sync.dma_start(out=w_raw[0][:], in_=w_rows[0])
+        for i in (2, 3):
+            for h in range(2):
+                load_x(i, h)
+        nc.sync.dma_start(slot_sb[:], slot)
+        nc.sync.dma_start(out=store[0][:], in_=mem[0:P, :])
+        nc.sync.dma_start(out=w_raw[1][:], in_=w_rows[1])
+        nc.sync.dma_start(out=store[1][:], in_=mem[P : 2 * P, :])
+
+        pairs = [keep.tile([P, T, 2], BF16, name="pairs%d" % i, align_bytes=64) for i in range(4)]
+        picked = [keep.tile([P, 2, S], U32, name="picked%d" % z, align_bytes=64) for z in range(2)]
+        grouped = [keep.tile([P, S * 4], BF16, name="grouped%d" % z, align_bytes=64) for z in range(2)]
+        x_codes = [keep.tile([P, S], U32, name="x_codes%d" % z, align_bytes=64) for z in range(2)]
+        x_scales = [keep.tile([P, S], U8, name="x_scales%d" % z, align_bytes=64) for z in range(2)]
+        w_grouped = [keep.tile([P, N * 4], BF16, name="w_grouped%d" % z, align_bytes=64) for z in range(2)]
+        w_codes = [keep.tile([P, N], U32, name="w_codes%d" % z, align_bytes=64) for z in range(2)]
+        w_scales = [keep.tile([P, N], U8, name="w_scales%d" % z, align_bytes=64) for z in range(2)]
+        old = [keep.tile([P, S], F32, name="old%d" % b) for b in range(2)]
+        new = [keep.tile([P, S], F32, name="new%d" % b) for b in range(2)]
+        acc = [psum.tile([P, S], F32, name="acc%d" % b) for b in range(2)]
+
+        def cast_scalar(i, src, t0, lo, hi):
+            nc.scalar.copy(out=pairs[i][:, t0 + lo : t0 + hi, :], in_=src[:, :, lo:hi].rearrange("p e t -> p t e"))
+
+        def cast_vector(i, src, t0, lo, hi):
+            nc.vector.tensor_copy(out=pairs[i][:, t0 + lo : t0 + hi, :], in_=src[:, :, lo:hi].rearrange("p e t -> p t e"))
+
+        def gather(i, lo, hi):
+            window = pairs[i][:].rearrange("p t e -> p (t e)").bitcast(U32)
+            nc.vector.tensor_copy(picked[i // 2][:, i % 2, lo:hi], window.indirect(offs_sb[:, lo // 16 : hi // 16]))
+
+        def weave_args(z, lo, hi, dt):
+            dst = grouped[z][:, 4 * lo : 4 * hi].bitcast(dt).rearrange("p (s u) -> p s u", u=2)
+            src = picked[z][:, :, lo:hi].bitcast(dt).rearrange("p u s -> p s u")
+            return dst, src
+
+        def quantize_x(z, lo, hi):
+            nc.vector.quantize_mx(out=x_codes[z][:, lo:hi].bitcast(FP8X4), scales=x_scales[z][:, lo:hi], in_=grouped[z][:, 4 * lo : 4 * hi])
+
+        def interleave_w(z, lo, hi):
+            nc.scalar.copy(
+                out=w_grouped[z][:, 4 * lo : 4 * hi].rearrange("p (c i j) -> p c j i", i=4, j=4),
+                in_=w_raw[z][:, :, lo:hi].rearrange("p j (c i) -> p c j i", i=4),
+            )
+
+        def quantize_w(z, lo, hi):
+            nc.vector.quantize_mx(out=w_codes[z][:, lo:hi].bitcast(FP8X4), scales=w_scales[z][:, lo:hi], in_=w_grouped[z][:, 4 * lo : 4 * hi])
+
+        def multiply(z, b):
+            cols = slice(b * P, (b + 1) * P)
+            nc.tensor.matmul_mx(
+                out=acc[b][:],
+                lhsT=w_codes[z][:, cols].bitcast(FP8X4),
+                lhsT_scale=w_scales[z][:, cols],
+                rhs=x_codes[z][:].bitcast(FP8X4),
+                rhs_scale=x_scales[z][:],
+                start=(z == 0),
+                stop=(z == 1),
+            )
+
+        ident = keep.tile([P, P], F32, name="ident")
+        make_identity(nc, ident[:])
+        y1 = keep.tile([P, S], F32, name="y1")
+        turned = keep.tile([P, S], F32, name="turned")
+        sum_t = psum.tile([P, S], F32, name="sum_t")
+        sum_back = psum.tile([P, S], F32, name="sum_back")
+
+        for i in range(2):
+            cast_scalar(i, raw[i][0], 0, 0, 512)
+            cast_vector(i, raw[i][1], 512, 0, 512)
+            gather(i, 0, S)
+        dst, src = weave_args(0, 0, S, mybir.dt.int32)
+        nc.vector.tensor_copy(out=dst, in_=src)
+        interleave_w(0, 0, N)
+        quantize_w(0, 0, N)
+        quantize_x(0, 0, S)
+        for b in range(2):
+            multiply(0, b)
+        cast_scalar(2, raw[2][0], 0, 0, 512)
+        cast_vector(2, raw[2][1], 512, 0, 512)
+        gather(2, 0, S)
+        cast_scalar(3, raw[3][0], 0, 0, 512)
+        cast_vector(3, raw[3][1], 512, 0, 352)
+        cast_scalar(3, raw[3][1], 512, 352, 512)
+        for h in range(2):
+            gather(3, h * 256, (h + 1) * 256)
+            dst, src = weave_args(1, h * 256, (h + 1) * 256, U32)
+            nc.scalar.copy(out=dst, in_=src)
+        quantize_x(1, 0, 256)
+        nc.vector.tensor_copy(old[0][:], store[0][:].indirect(slot_sb[:]))
+        quantize_x(1, 256, 512)
+        for b in range(2):
+            interleave_w(1, b * P, (b + 1) * P)
+        quantize_w(1, 0, P)
+        multiply(1, 0)
+        nc.vector.tensor_copy(old[1][:, 0:256], store[1][:].indirect(slot_sb[:, 0:16]))
+        nc.vector.tensor_tensor(new[0][:], acc[0][:], old[0][:], ADD)
+        quantize_w(1, P, 2 * P)
+        multiply(1, 1)
+        nc.vector.tensor_copy(old[1][:, 256:512], store[1][:].indirect(slot_sb[:, 16:32]))
+        nc.scalar.copy(out=y1[:], in_=acc[1][:])
+        for c in range(4):
+            cols = slice(c * P, (c + 1) * P)
+            nc.tensor.matmul(sum_t[:, cols], y1[:, cols], ident[:], start=True, stop=False, is_transpose=True)
+            nc.tensor.matmul(sum_t[:, cols], old[1][:, cols], ident[:], start=False, stop=True, is_transpose=True)
+        nc.scalar.copy(out=turned[:], in_=sum_t[:])
+        for c in range(4):
+            cols = slice(c * P, (c + 1) * P)
+            nc.tensor.transpose(sum_back[:, cols], turned[:, cols], ident[:])
+        nc.scalar.copy(out=new[1][:], in_=sum_back[:])
+        for b in range(2):
+            nc.vector.tensor_copy(store[b][:].indirect(slot_sb[:]), new[b][:])
+            nc.sync.dma_start(out=out[b * P : (b + 1) * P, :], in_=store[b][:])

@@ -29,22 +29,17 @@ def tile_picked_idxput_add_e_kernel(tc, xT, mem, w1, offs, slot, out):
         offs_sb = keep.tile([P, S // 16], U16, name="offs_sb")
         slot_sb = keep.tile([P, S // 16], U16, name="slot_sb")
 
-        raw = [[keep.tile([P, 2, T // 2], F32, name="raw%d_%d" % (i, h)) for h in range(2)] for i in range(4)]
-        w_raw = [keep.tile([P, 4, N], F32, name="w_raw%d" % z) for z in range(2)]
+        widths = [T, T, T // 2, T // 2]
+        raw = [[keep.tile([P, 2, widths[i]], F32, name="raw%d_%d" % (i, h), tag="raw%d_%d" % (i, h), align_bytes=64) for h in range(T // widths[i])] for i in range(4)]
+        w_raw = [keep.tile([P, 4, N], F32, name="w_raw%d" % z, tag="wr%d" % z, align_bytes=64) for z in range(2)]
         store = [keep.tile([P, U], F32, name="store%d" % b) for b in range(2)]
 
-        def load_x(i, h):
-            nc.sync.dma_start(out=raw[i][h][:], in_=x_pairs[i // 2, i % 2][:, :, h * 512 : (h + 1) * 512])
-
-        load_x(0, 0)
-        load_x(0, 1)
-        nc.sync.dma_start(offs_sb[:], offs)
-        load_x(1, 0)
-        load_x(1, 1)
+        for i in range(4):
+            for h in range(T // widths[i]):
+                nc.sync.dma_start(out=raw[i][h][:], in_=x_pairs[i // 2, i % 2][:, :, h * widths[i] : (h + 1) * widths[i]])
+            if i == 0:
+                nc.sync.dma_start(offs_sb[:], offs)
         nc.sync.dma_start(out=w_raw[0][:], in_=w_rows[0])
-        for i in (2, 3):
-            for h in range(2):
-                load_x(i, h)
         nc.sync.dma_start(slot_sb[:], slot)
         nc.sync.dma_start(out=store[0][:], in_=mem[0:P, :])
         nc.sync.dma_start(out=w_raw[1][:], in_=w_rows[1])
@@ -52,33 +47,36 @@ def tile_picked_idxput_add_e_kernel(tc, xT, mem, w1, offs, slot, out):
 
         pairs = [keep.tile([P, T, 2], BF16, name="pairs%d" % i, align_bytes=64) for i in range(4)]
         picked = [keep.tile([P, 2, S], U32, name="picked%d" % z, align_bytes=64) for z in range(2)]
-        grouped = [keep.tile([P, S * 4], BF16, name="grouped%d" % z, align_bytes=64) for z in range(2)]
-        x_codes = [keep.tile([P, S], U32, name="x_codes%d" % z, align_bytes=64) for z in range(2)]
+        grouped = []
+        x_codes = []
         x_scales = [keep.tile([P, S], U8, name="x_scales%d" % z, align_bytes=64) for z in range(2)]
-        w_grouped = [keep.tile([P, N * 4], BF16, name="w_grouped%d" % z, align_bytes=64) for z in range(2)]
-        w_codes = [keep.tile([P, N], U32, name="w_codes%d" % z, align_bytes=64) for z in range(2)]
+        w_grouped = [keep.tile([P, N * 4], BF16, name="w_grouped%d" % z, tag="wg%d" % z, align_bytes=64) for z in range(2)]
+        w_codes = [keep.tile([P, N], U32, name="w_codes%d" % z, tag="wc%d" % z, align_bytes=64) for z in range(2)]
         w_scales = [keep.tile([P, N], U8, name="w_scales%d" % z, align_bytes=64) for z in range(2)]
-        old = [keep.tile([P, S], F32, name="old%d" % b) for b in range(2)]
+        old0 = keep.tile([P, S], F32, name="old0")
         new = [keep.tile([P, S], F32, name="new%d" % b) for b in range(2)]
-        acc = [psum.tile([P, S], F32, name="acc%d" % b) for b in range(2)]
+        acc = [psum.tile([P, S], F32, name="acc%d" % b, tag="acc%d" % b) for b in range(2)]
+        ident = keep.tile([P, P], F32, name="ident")
+        make_identity(nc, ident[:])
+        y1 = keep.tile([P, S], F32, name="y1")
+        turned = keep.tile([P, S], F32, name="turned")
+        sum_t = [psum.tile([P, P], F32, name="sum_t%d" % c) for c in range(4)]
+        sum_back = [psum.tile([P, S // 2], F32, name="sum_back%d" % h) for h in range(2)]
 
-        def cast_scalar(i, src, t0, lo, hi):
-            nc.scalar.copy(out=pairs[i][:, t0 + lo : t0 + hi, :], in_=src[:, :, lo:hi].rearrange("p e t -> p t e"))
+        def cast(u, h, share):
+            width = widths[u]
+            t0 = h * width
+            if share > 0:
+                nc.scalar.copy(out=pairs[u][:, t0 : t0 + share, :], in_=raw[u][h][:, :, 0:share].rearrange("p e t -> p t e"))
+            if share < width:
+                nc.vector.tensor_copy(out=pairs[u][:, t0 + share : t0 + width, :], in_=raw[u][h][:, :, share:width].rearrange("p e t -> p t e"))
 
-        def cast_vector(i, src, t0, lo, hi):
-            nc.vector.tensor_copy(out=pairs[i][:, t0 + lo : t0 + hi, :], in_=src[:, :, lo:hi].rearrange("p e t -> p t e"))
+        def gather(u, lo, hi):
+            window = pairs[u][:].rearrange("p t e -> p (t e)").bitcast(U32)
+            nc.vector.tensor_copy(picked[u // 2][:, u % 2, lo:hi], window.indirect(offs_sb[:, lo // 16 : hi // 16]))
 
-        def gather(i, lo, hi):
-            window = pairs[i][:].rearrange("p t e -> p (t e)").bitcast(U32)
-            nc.vector.tensor_copy(picked[i // 2][:, i % 2, lo:hi], window.indirect(offs_sb[:, lo // 16 : hi // 16]))
-
-        def weave_args(z, lo, hi, dt):
-            dst = grouped[z][:, 4 * lo : 4 * hi].bitcast(dt).rearrange("p (s u) -> p s u", u=2)
-            src = picked[z][:, :, lo:hi].bitcast(dt).rearrange("p u s -> p s u")
-            return dst, src
-
-        def quantize_x(z, lo, hi):
-            nc.vector.quantize_mx(out=x_codes[z][:, lo:hi].bitcast(FP8X4), scales=x_scales[z][:, lo:hi], in_=grouped[z][:, 4 * lo : 4 * hi])
+        def quantize_x(z):
+            nc.vector.quantize_mx(out=x_codes[z][:].bitcast(FP8X4), scales=x_scales[z][:], in_=grouped[z][:])
 
         def interleave_w(z, lo, hi):
             nc.scalar.copy(
@@ -101,56 +99,64 @@ def tile_picked_idxput_add_e_kernel(tc, xT, mem, w1, offs, slot, out):
                 stop=(z == 1),
             )
 
-        ident = keep.tile([P, P], F32, name="ident")
-        make_identity(nc, ident[:])
-        y1 = keep.tile([P, S], F32, name="y1")
-        turned = keep.tile([P, S], F32, name="turned")
-        sum_t = psum.tile([P, S], F32, name="sum_t")
-        sum_back = psum.tile([P, S], F32, name="sum_back")
-
-        for i in range(2):
-            cast_scalar(i, raw[i][0], 0, 0, 512)
-            cast_vector(i, raw[i][1], 512, 0, 512)
-            gather(i, 0, S)
-        dst, src = weave_args(0, 0, S, mybir.dt.int32)
-        nc.vector.tensor_copy(out=dst, in_=src)
+        cast(0, 0, 384)
+        gather(0, 0, S)
+        cast(1, 0, 384)
+        gather(1, 0, S)
+        cast(2, 0, 512)
+        cast(2, 1, 256)
+        grouped.append(keep.tile([P, S * 4], BF16, name="grouped0", tag="raw2_0", align_bytes=64))
+        nc.vector.tensor_copy(
+            out=grouped[0][:].bitcast(mybir.dt.int32).rearrange("p (s u) -> p s u", u=2),
+            in_=picked[0][:].bitcast(mybir.dt.int32).rearrange("p u s -> p s u"),
+        )
+        gather(2, 0, S)
+        cast(3, 0, 512)
+        cast(3, 1, 320)
+        x_codes.append(keep.tile([P, S], U32, name="x_codes0", tag="raw3_0", align_bytes=64))
+        x_codes.append(keep.tile([P, S], U32, name="x_codes1", align_bytes=64))
+        quantize_x(0)
         interleave_w(0, 0, N)
+        grouped.append(keep.tile([P, S * 4], BF16, name="grouped1", tag="wr0", align_bytes=64))
+        for h in range(2):
+            lo, hi = h * 256, (h + 1) * 256
+            gather(3, lo, hi)
+            nc.scalar.copy(
+                out=grouped[1][:, 4 * lo : 4 * hi].bitcast(U32).rearrange("p (s u) -> p s u", u=2),
+                in_=picked[1][:, :, lo:hi].rearrange("p u s -> p s u"),
+            )
+        nc.vector.tensor_copy(old0[:], store[0][:].indirect(slot_sb[:]))
         quantize_w(0, 0, N)
-        quantize_x(0, 0, S)
         for b in range(2):
             multiply(0, b)
-        cast_scalar(2, raw[2][0], 0, 0, 512)
-        cast_vector(2, raw[2][1], 512, 0, 512)
-        gather(2, 0, S)
-        cast_scalar(3, raw[3][0], 0, 0, 512)
-        cast_vector(3, raw[3][1], 512, 0, 352)
-        cast_scalar(3, raw[3][1], 512, 352, 512)
-        for h in range(2):
-            gather(3, h * 256, (h + 1) * 256)
-            dst, src = weave_args(1, h * 256, (h + 1) * 256, U32)
-            nc.scalar.copy(out=dst, in_=src)
-        quantize_x(1, 0, 256)
-        nc.vector.tensor_copy(old[0][:], store[0][:].indirect(slot_sb[:]))
-        quantize_x(1, 256, 512)
-        for b in range(2):
-            interleave_w(1, b * P, (b + 1) * P)
+        quantize_x(1)
+        interleave_w(1, 0, P)
+        interleave_w(1, P, N)
         quantize_w(1, 0, P)
         multiply(1, 0)
-        nc.vector.tensor_copy(old[1][:, 0:256], store[1][:].indirect(slot_sb[:, 0:16]))
-        nc.vector.tensor_tensor(new[0][:], acc[0][:], old[0][:], ADD)
-        quantize_w(1, P, 2 * P)
+        quantize_w(1, P, N)
         multiply(1, 1)
-        nc.vector.tensor_copy(old[1][:, 256:512], store[1][:].indirect(slot_sb[:, 16:32]))
-        nc.scalar.copy(out=y1[:], in_=acc[1][:])
+        old1a = keep.tile([P, 384], F32, name="old1a", tag="wr1", align_bytes=64)
+        nc.vector.tensor_copy(old1a[:], store[1][:].indirect(slot_sb[:, 0:24]))
+        nc.vector.tensor_tensor(new[0][:], acc[0][:], old0[:], ADD)
+        old1b = keep.tile([P, P], F32, name="old1b", tag="wc1", align_bytes=64)
+        nc.vector.tensor_copy(old1b[:], store[1][:].indirect(slot_sb[:, 24:32]))
+        old1 = [old1a[:, c * P : (c + 1) * P] for c in range(3)] + [old1b[:]]
+        for h in range(2):
+            nc.scalar.copy(out=y1[:, h * 256 : (h + 1) * 256], in_=acc[1][:, h * 256 : (h + 1) * 256])
+        for c in range(3):
+            nc.tensor.matmul(sum_t[c][:], old1[c], ident[:], start=True, stop=False, is_transpose=True)
         for c in range(4):
             cols = slice(c * P, (c + 1) * P)
-            nc.tensor.matmul(sum_t[:, cols], y1[:, cols], ident[:], start=True, stop=False, is_transpose=True)
-            nc.tensor.matmul(sum_t[:, cols], old[1][:, cols], ident[:], start=False, stop=True, is_transpose=True)
-        nc.scalar.copy(out=turned[:], in_=sum_t[:])
-        for c in range(4):
-            cols = slice(c * P, (c + 1) * P)
-            nc.tensor.transpose(sum_back[:, cols], turned[:, cols], ident[:])
-        nc.scalar.copy(out=new[1][:], in_=sum_back[:])
+            nc.tensor.matmul(sum_t[c][:], y1[:, cols], ident[:], start=(c == 3), stop=(c < 3), is_transpose=True)
+            if c == 3:
+                nc.tensor.matmul(sum_t[c][:], old1[c], ident[:], start=False, stop=True, is_transpose=True)
+            nc.scalar.copy(out=turned[:, cols], in_=sum_t[c][:])
+        for h in range(2):
+            for c in range(2):
+                cols = slice((2 * h + c) * P, (2 * h + c + 1) * P)
+                nc.tensor.transpose(sum_back[h][:, c * P : (c + 1) * P], turned[:, cols], ident[:])
+            nc.scalar.copy(out=new[1][:, h * 256 : (h + 1) * 256], in_=sum_back[h][:])
         for b in range(2):
             nc.vector.tensor_copy(store[b][:].indirect(slot_sb[:]), new[b][:])
             nc.sync.dma_start(out=out[b * P : (b + 1) * P, :], in_=store[b][:])

@@ -1,7 +1,6 @@
 from contextlib import ExitStack
 
 import concourse.mybir as mybir
-from concourse.masks import make_identity
 
 K, T, S, N, U = 1024, 1024, 512, 256, 1024
 FLOPS = 2 * K * N * S
@@ -54,14 +53,8 @@ def tile_picked_idxput_add_e_kernel(tc, xT, mem, w1, offs, slot, out):
         w_codes = [keep.tile([P, N], U32, name="w_codes%d" % z, tag="wc%d" % z, align_bytes=64) for z in range(2)]
         w_scales = [keep.tile([P, N], U8, name="w_scales%d" % z, align_bytes=64) for z in range(2)]
         old0 = keep.tile([P, S], F32, name="old0")
-        new = [keep.tile([P, S], F32, name="new%d" % b) for b in range(2)]
+        y = [keep.tile([P, S], F32, name="y%d" % b) for b in range(2)]
         acc = [psum.tile([P, S], F32, name="acc%d" % b, tag="acc%d" % b) for b in range(2)]
-        ident = keep.tile([P, P], F32, name="ident")
-        make_identity(nc, ident[:])
-        y1 = keep.tile([P, S], F32, name="y1")
-        turned = keep.tile([P, S], F32, name="turned")
-        sum_t = [psum.tile([P, P], F32, name="sum_t%d" % c) for c in range(4)]
-        sum_back = [psum.tile([P, S // 2], F32, name="sum_back%d" % h) for h in range(2)]
 
         def cast(u, h, share):
             width = widths[u]
@@ -136,27 +129,10 @@ def tile_picked_idxput_add_e_kernel(tc, xT, mem, w1, offs, slot, out):
         multiply(1, 0)
         quantize_w(1, P, N)
         multiply(1, 1)
-        old1a = keep.tile([P, 384], F32, name="old1a", tag="wr1", align_bytes=64)
-        nc.vector.tensor_copy(old1a[:], store[1][:].indirect(slot_sb[:, 0:24]))
-        nc.vector.tensor_tensor(new[0][:], acc[0][:], old0[:], ADD)
-        old1b = keep.tile([P, P], F32, name="old1b", tag="wc1", align_bytes=64)
-        nc.vector.tensor_copy(old1b[:], store[1][:].indirect(slot_sb[:, 24:32]))
-        old1 = [old1a[:, c * P : (c + 1) * P] for c in range(3)] + [old1b[:]]
-        for h in range(2):
-            nc.scalar.copy(out=y1[:, h * 256 : (h + 1) * 256], in_=acc[1][:, h * 256 : (h + 1) * 256])
-        for c in range(3):
-            nc.tensor.matmul(sum_t[c][:], old1[c], ident[:], start=True, stop=False, is_transpose=True)
-        for c in range(4):
-            cols = slice(c * P, (c + 1) * P)
-            nc.tensor.matmul(sum_t[c][:], y1[:, cols], ident[:], start=(c == 3), stop=(c < 3), is_transpose=True)
-            if c == 3:
-                nc.tensor.matmul(sum_t[c][:], old1[c], ident[:], start=False, stop=True, is_transpose=True)
-            nc.scalar.copy(out=turned[:, cols], in_=sum_t[c][:])
-        for h in range(2):
-            for c in range(2):
-                cols = slice((2 * h + c) * P, (2 * h + c + 1) * P)
-                nc.tensor.transpose(sum_back[h][:, c * P : (c + 1) * P], turned[:, cols], ident[:])
-            nc.scalar.copy(out=new[1][:, h * 256 : (h + 1) * 256], in_=sum_back[h][:])
+        old1 = keep.tile([P, S], F32, name="old1", tag="wr1", align_bytes=64)
+        nc.vector.tensor_copy(old1[:], store[1][:].indirect(slot_sb[:]))
+        old = [old0, old1]
         for b in range(2):
-            nc.vector.tensor_copy(store[b][:].indirect(slot_sb[:]), new[b][:])
+            nc.scalar.copy(out=y[b][:], in_=acc[b][:])
+            nc.vector.tensor_tensor(store[b][:].indirect(slot_sb[:]), old[b][:], y[b][:], ADD)
             nc.sync.dma_start(out=out[b * P : (b + 1) * P, :], in_=store[b][:])

@@ -7,6 +7,7 @@ FLOPS = 2 * K * N * S
 
 F32 = mybir.dt.float32
 BF16 = mybir.dt.bfloat16
+I32 = mybir.dt.int32
 U32 = mybir.dt.uint32
 U16 = mybir.dt.uint16
 U8 = mybir.dt.uint8
@@ -14,6 +15,9 @@ FP8X4 = mybir.dt.float8_e4m3fn_x4
 ADD = mybir.AluOpType.add
 
 P = 128
+H = S // 2
+FIRST = 192
+WIDTHS = [T, T, T // 2, T // 2]
 
 
 def tile_picked_idxput_add_e_kernel(tc, xT, mem, w1, offs, slot, out):
@@ -27,112 +31,120 @@ def tile_picked_idxput_add_e_kernel(tc, xT, mem, w1, offs, slot, out):
 
         offs_sb = keep.tile([P, S // 16], U16, name="offs_sb")
         slot_sb = keep.tile([P, S // 16], U16, name="slot_sb")
-
-        widths = [T, T, T // 2, T // 2]
-        raw = [[keep.tile([P, 2, widths[i]], F32, name="raw%d_%d" % (i, h), tag="raw%d_%d" % (i, h), align_bytes=64) for h in range(T // widths[i])] for i in range(4)]
-        w_raw = [keep.tile([P, 4, N], F32, name="w_raw%d" % z, tag="wr%d" % z, align_bytes=64) for z in range(2)]
+        raw = [[keep.tile([P, 2, WIDTHS[i]], F32, name="raw%d_%d" % (i, h), tag="raw%d_%d" % (i, h), align_bytes=64) for h in range(T // WIDTHS[i])] for i in range(4)]
+        w_raw = [[keep.tile([P, 4, P], F32, name="w_raw%d%d" % (b, z), tag="wr%d%d" % (b, z), align_bytes=64) for z in range(2)] for b in range(2)]
         store = [keep.tile([P, U], F32, name="store%d" % b) for b in range(2)]
 
         for i in range(4):
-            for h in range(T // widths[i]):
-                nc.sync.dma_start(out=raw[i][h][:], in_=x_pairs[i // 2, i % 2][:, :, h * widths[i] : (h + 1) * widths[i]])
+            for h in range(T // WIDTHS[i]):
+                nc.sync.dma_start(out=raw[i][h][:], in_=x_pairs[i // 2, i % 2][:, :, h * WIDTHS[i] : (h + 1) * WIDTHS[i]])
             if i == 0:
                 nc.sync.dma_start(offs_sb[:], offs)
-        nc.sync.dma_start(out=w_raw[0][:], in_=w_rows[0])
-        nc.sync.dma_start(slot_sb[:], slot)
-        nc.sync.dma_start(out=store[0][:], in_=mem[0:P, :])
-        nc.sync.dma_start(out=w_raw[1][:], in_=w_rows[1])
-        nc.sync.dma_start(out=store[1][:], in_=mem[P : 2 * P, :])
+                nc.sync.dma_start(slot_sb[:], slot)
+        for z in range(2):
+            nc.sync.dma_start(out=w_raw[0][z][:], in_=w_rows[z][:, :, 0:P])
+            nc.sync.dma_start(out=store[z][:], in_=mem[z * P : (z + 1) * P, :])
+        for z in range(2):
+            nc.sync.dma_start(out=w_raw[1][z][:], in_=w_rows[z][:, :, P:N])
 
         pairs = [keep.tile([P, T, 2], BF16, name="pairs%d" % i, align_bytes=64) for i in range(4)]
         picked = [keep.tile([P, 2, S], U32, name="picked%d" % z, align_bytes=64) for z in range(2)]
-        grouped = []
-        x_codes = []
         x_scales = [keep.tile([P, S], U8, name="x_scales%d" % z, align_bytes=64) for z in range(2)]
-        w_grouped = [keep.tile([P, N * 4], BF16, name="w_grouped%d" % z, tag="wg%d" % z, align_bytes=64) for z in range(2)]
-        w_codes = [keep.tile([P, N], U32, name="w_codes%d" % z, tag="wc%d" % z, align_bytes=64) for z in range(2)]
-        w_scales = [keep.tile([P, N], U8, name="w_scales%d" % z, align_bytes=64) for z in range(2)]
-        old0 = keep.tile([P, S], F32, name="old0")
-        y = [keep.tile([P, S], F32, name="y%d" % b) for b in range(2)]
-        acc = [psum.tile([P, S], F32, name="acc%d" % b, tag="acc%d" % b) for b in range(2)]
+        w_codes = [keep.tile([P, 2 * P], U32, name="w_codes%d" % b, tag="wc%d" % b, align_bytes=64) for b in range(2)]
+        w_scales = [keep.tile([P, 2 * P], U8, name="w_scales%d" % b, align_bytes=64) for b in range(2)]
+        acc = [[psum.tile([P, H], F32, name="acc%d%d" % (b, h)) for h in range(2)] for b in range(2)]
 
-        def cast(u, h, share):
-            width = widths[u]
+        def cast(i, h, share):
+            width = WIDTHS[i]
             t0 = h * width
-            if share > 0:
-                nc.scalar.copy(out=pairs[u][:, t0 : t0 + share, :], in_=raw[u][h][:, :, 0:share].rearrange("p e t -> p t e"))
+            nc.scalar.copy(out=pairs[i][:, t0 : t0 + share, :], in_=raw[i][h][:, :, 0:share].rearrange("p e t -> p t e"))
             if share < width:
-                nc.vector.tensor_copy(out=pairs[u][:, t0 + share : t0 + width, :], in_=raw[u][h][:, :, share:width].rearrange("p e t -> p t e"))
+                nc.vector.tensor_copy(out=pairs[i][:, t0 + share : t0 + width, :], in_=raw[i][h][:, :, share:width].rearrange("p e t -> p t e"))
 
-        def gather(u, lo, hi):
-            window = pairs[u][:].rearrange("p t e -> p (t e)").bitcast(U32)
-            nc.vector.tensor_copy(picked[u // 2][:, u % 2, lo:hi], window.indirect(offs_sb[:, lo // 16 : hi // 16]))
+        def gather(i, lo, hi):
+            window = pairs[i][:].rearrange("p t e -> p (t e)").bitcast(U32)
+            nc.vector.tensor_copy(picked[i // 2][:, i % 2, lo:hi], window.indirect(offs_sb[:, lo // 16 : hi // 16]))
 
-        def quantize_x(z):
-            nc.vector.quantize_mx(out=x_codes[z][:].bitcast(FP8X4), scales=x_scales[z][:], in_=grouped[z][:])
-
-        def interleave_w(z, lo, hi):
+        def interleave_w(b, z, tag):
+            grouped = keep.tile([P, 4 * P], BF16, name="w_grouped%d%d" % (b, z), tag=tag, align_bytes=64)
             nc.scalar.copy(
-                out=w_grouped[z][:, 4 * lo : 4 * hi].rearrange("p (c i j) -> p c j i", i=4, j=4),
-                in_=w_raw[z][:, :, lo:hi].rearrange("p j (c i) -> p c j i", i=4),
+                out=grouped[:].rearrange("p (c i j) -> p c j i", i=4, j=4),
+                in_=w_raw[b][z][:].rearrange("p j (c i) -> p c j i", i=4),
             )
+            return grouped
 
-        def quantize_w(z, lo, hi):
-            nc.vector.quantize_mx(out=w_codes[z][:, lo:hi].bitcast(FP8X4), scales=w_scales[z][:, lo:hi], in_=w_grouped[z][:, 4 * lo : 4 * hi])
+        def quantize_w(b, z, grouped):
+            cols = slice(z * P, (z + 1) * P)
+            nc.vector.quantize_mx(out=w_codes[b][:, cols].bitcast(FP8X4), scales=w_scales[b][:, cols], in_=grouped[:])
 
-        def multiply(z, b):
-            cols = slice(b * P, (b + 1) * P)
+        def multiply(acc, b, z, lo, hi):
+            cols = slice(z * P, (z + 1) * P)
             nc.tensor.matmul_mx(
-                out=acc[b][:],
-                lhsT=w_codes[z][:, cols].bitcast(FP8X4),
-                lhsT_scale=w_scales[z][:, cols],
-                rhs=x_codes[z][:].bitcast(FP8X4),
-                rhs_scale=x_scales[z][:],
+                out=acc[:],
+                lhsT=w_codes[b][:, cols].bitcast(FP8X4),
+                lhsT_scale=w_scales[b][:, cols],
+                rhs=x_codes[z][:, lo:hi].bitcast(FP8X4),
+                rhs_scale=x_scales[z][:, lo:hi],
                 start=(z == 0),
                 stop=(z == 1),
             )
 
-        cast(0, 0, 384)
-        gather(0, 0, S)
-        cast(1, 0, 384)
-        gather(1, 0, S)
+        def put(b, y, lo, hi):
+            nc.vector.tensor_tensor(store[b][:].indirect(slot_sb[:, lo // 16 : hi // 16]), old[b][:, lo:hi], y[:], ADD)
+
+        for i in range(2):
+            cast(i, 0, 336)
+            gather(i, 0, S)
         cast(2, 0, 512)
-        cast(2, 1, 256)
-        grouped.append(keep.tile([P, S * 4], BF16, name="grouped0", tag="raw2_0", align_bytes=64))
+        cast(2, 1, 224)
+        grouped0 = keep.tile([P, S * 4], BF16, name="grouped0", tag="raw2_0", align_bytes=64)
         nc.vector.tensor_copy(
-            out=grouped[0][:].bitcast(mybir.dt.int32).rearrange("p (s u) -> p s u", u=2),
-            in_=picked[0][:].bitcast(mybir.dt.int32).rearrange("p u s -> p s u"),
+            out=grouped0[:].bitcast(I32).rearrange("p (s u) -> p s u", u=2),
+            in_=picked[0][:].bitcast(I32).rearrange("p u s -> p s u"),
         )
         gather(2, 0, S)
         cast(3, 0, 512)
-        cast(3, 1, 320)
-        x_codes.append(keep.tile([P, S], U32, name="x_codes0", tag="raw3_0", align_bytes=64))
-        x_codes.append(keep.tile([P, S], U32, name="x_codes1", align_bytes=64))
-        quantize_x(0)
-        interleave_w(0, 0, N)
-        grouped.append(keep.tile([P, S * 4], BF16, name="grouped1", tag="wr0", align_bytes=64))
-        for h in range(2):
-            lo, hi = h * 256, (h + 1) * 256
-            gather(3, lo, hi)
+        cast(3, 1, 208)
+        x_codes = [
+            keep.tile([P, S], U32, name="x_codes0", tag="raw3_0", align_bytes=64),
+            keep.tile([P, S], U32, name="x_codes1", align_bytes=64),
+        ]
+        nc.vector.quantize_mx(out=x_codes[0][:].bitcast(FP8X4), scales=x_scales[0][:], in_=grouped0[:])
+        gather(3, 0, H)
+        gather(3, H, S)
+        w00 = interleave_w(0, 0, "wg00")
+        grouped1 = keep.tile([P, S * 4], BF16, name="grouped1", align_bytes=64)
+        for lo in (0, H):
             nc.scalar.copy(
-                out=grouped[1][:, 4 * lo : 4 * hi].bitcast(U32).rearrange("p (s u) -> p s u", u=2),
-                in_=picked[1][:, :, lo:hi].rearrange("p u s -> p s u"),
+                out=grouped1[:, 4 * lo : 4 * (lo + H)].bitcast(U32).rearrange("p (s u) -> p s u", u=2),
+                in_=picked[1][:, :, lo : lo + H].rearrange("p u s -> p s u"),
             )
-        nc.vector.tensor_copy(old0[:], store[0][:].indirect(slot_sb[:]))
-        quantize_w(0, 0, N)
-        for b in range(2):
-            multiply(0, b)
-        quantize_x(1)
-        interleave_w(1, 0, P)
-        interleave_w(1, P, N)
-        quantize_w(1, 0, P)
-        multiply(1, 0)
-        quantize_w(1, P, N)
-        multiply(1, 1)
-        old1 = keep.tile([P, S], F32, name="old1", tag="wr1", align_bytes=64)
-        nc.vector.tensor_copy(old1[:], store[1][:].indirect(slot_sb[:]))
-        old = [old0, old1]
-        for b in range(2):
-            nc.scalar.copy(out=y[b][:], in_=acc[b][:])
-            nc.vector.tensor_tensor(store[b][:].indirect(slot_sb[:]), old[b][:], y[b][:], ADD)
-            nc.sync.dma_start(out=out[b * P : (b + 1) * P, :], in_=store[b][:])
+        quantize_w(0, 0, w00)
+        old = [keep.tile([P, S], F32, name="old0")]
+        nc.vector.tensor_copy(old[0][:], store[0][:].indirect(slot_sb[:]))
+        nc.vector.quantize_mx(out=x_codes[1][:].bitcast(FP8X4), scales=x_scales[1][:], in_=grouped1[:])
+        quantize_w(0, 1, interleave_w(0, 1, "wg01"))
+        old.append(keep.tile([P, S], F32, name="old1", tag="wr01", align_bytes=64))
+        nc.vector.tensor_copy(old[1][:], store[1][:].indirect(slot_sb[:]))
+        w10 = interleave_w(1, 0, "wg10")
+        for z in range(2):
+            for h in range(2):
+                multiply(acc[0][h], 0, z, h * H, (h + 1) * H)
+        y0a = keep.tile([P, FIRST], F32, name="y0a")
+        nc.scalar.copy(out=y0a[:], in_=acc[0][0][:, 0:FIRST])
+        put(0, y0a, 0, FIRST)
+        quantize_w(1, 0, w10)
+        quantize_w(1, 1, interleave_w(1, 1, "wc0"))
+        y0b = keep.tile([P, S - FIRST], F32, name="y0b", tag="wr11", align_bytes=64)
+        nc.scalar.copy(out=y0b[:, 0 : H - FIRST], in_=acc[0][0][:, FIRST:H])
+        nc.scalar.copy(out=y0b[:, H - FIRST : S - FIRST], in_=acc[0][1][:])
+        put(0, y0b, FIRST, S)
+        nc.sync.dma_start(out=out[0:P, :], in_=store[0][:])
+        for z in range(2):
+            for h in range(2):
+                multiply(acc[1][h], 1, z, h * H, (h + 1) * H)
+        y1 = keep.tile([P, S], F32, name="y1")
+        for h in range(2):
+            nc.scalar.copy(out=y1[:, h * H : (h + 1) * H], in_=acc[1][h][:])
+        put(1, y1, 0, S)
+        nc.sync.dma_start(out=out[P:N, :], in_=store[1][:])

@@ -15,9 +15,12 @@ FP8X4 = mybir.dt.float8_e4m3fn_x4
 ADD = mybir.AluOpType.add
 
 P = 128
-H = S // 2
-FIRST = 192
+HALF = S // 2
 WIDTHS = [T, T, T // 2, T // 2]
+SHARE_WHOLE = 336
+SHARE_PAIR2 = 224
+SHARE_PAIR3 = 208
+FIRST = 192
 
 
 def tile_picked_idxput_add_e_kernel(tc, xT, mem, w1, offs, slot, out):
@@ -40,9 +43,10 @@ def tile_picked_idxput_add_e_kernel(tc, xT, mem, w1, offs, slot, out):
                 nc.sync.dma_start(out=raw[i][h][:], in_=x_pairs[i // 2, i % 2][:, :, h * WIDTHS[i] : (h + 1) * WIDTHS[i]])
             if i == 0:
                 nc.sync.dma_start(offs_sb[:], offs)
-                nc.sync.dma_start(slot_sb[:], slot)
         for z in range(2):
             nc.sync.dma_start(out=w_raw[0][z][:], in_=w_rows[z][:, :, 0:P])
+            if z == 0:
+                nc.sync.dma_start(slot_sb[:], slot)
             nc.sync.dma_start(out=store[z][:], in_=mem[z * P : (z + 1) * P, :])
         for z in range(2):
             nc.sync.dma_start(out=w_raw[1][z][:], in_=w_rows[z][:, :, P:N])
@@ -52,7 +56,7 @@ def tile_picked_idxput_add_e_kernel(tc, xT, mem, w1, offs, slot, out):
         x_scales = [keep.tile([P, S], U8, name="x_scales%d" % z, align_bytes=64) for z in range(2)]
         w_codes = [keep.tile([P, 2 * P], U32, name="w_codes%d" % b, tag="wc%d" % b, align_bytes=64) for b in range(2)]
         w_scales = [keep.tile([P, 2 * P], U8, name="w_scales%d" % b, align_bytes=64) for b in range(2)]
-        acc = [[psum.tile([P, H], F32, name="acc%d%d" % (b, h)) for h in range(2)] for b in range(2)]
+        acc = [[psum.tile([P, HALF], F32, name="acc%d%d" % (b, h)) for h in range(2)] for b in range(2)]
 
         def cast(i, h, share):
             width = WIDTHS[i]
@@ -77,47 +81,50 @@ def tile_picked_idxput_add_e_kernel(tc, xT, mem, w1, offs, slot, out):
             cols = slice(z * P, (z + 1) * P)
             nc.vector.quantize_mx(out=w_codes[b][:, cols].bitcast(FP8X4), scales=w_scales[b][:, cols], in_=grouped[:])
 
-        def multiply(acc, b, z, lo, hi):
-            cols = slice(z * P, (z + 1) * P)
-            nc.tensor.matmul_mx(
-                out=acc[:],
-                lhsT=w_codes[b][:, cols].bitcast(FP8X4),
-                lhsT_scale=w_scales[b][:, cols],
-                rhs=x_codes[z][:, lo:hi].bitcast(FP8X4),
-                rhs_scale=x_scales[z][:, lo:hi],
-                start=(z == 0),
-                stop=(z == 1),
-            )
+        def multiply(b):
+            for z in range(2):
+                cols = slice(z * P, (z + 1) * P)
+                for h in range(2):
+                    entries = slice(h * HALF, (h + 1) * HALF)
+                    nc.tensor.matmul_mx(
+                        out=acc[b][h][:],
+                        lhsT=w_codes[b][:, cols].bitcast(FP8X4),
+                        lhsT_scale=w_scales[b][:, cols],
+                        rhs=x_codes[z][:, entries].bitcast(FP8X4),
+                        rhs_scale=x_scales[z][:, entries],
+                        start=(z == 0),
+                        stop=(z == 1),
+                    )
 
         def put(b, y, lo, hi):
             nc.vector.tensor_tensor(store[b][:].indirect(slot_sb[:, lo // 16 : hi // 16]), old[b][:, lo:hi], y[:], ADD)
 
         for i in range(2):
-            cast(i, 0, 336)
+            cast(i, 0, SHARE_WHOLE)
             gather(i, 0, S)
-        cast(2, 0, 512)
-        cast(2, 1, 224)
+        cast(2, 0, WIDTHS[2])
+        cast(2, 1, SHARE_PAIR2)
         grouped0 = keep.tile([P, S * 4], BF16, name="grouped0", tag="raw2_0", align_bytes=64)
         nc.vector.tensor_copy(
             out=grouped0[:].bitcast(I32).rearrange("p (s u) -> p s u", u=2),
             in_=picked[0][:].bitcast(I32).rearrange("p u s -> p s u"),
         )
         gather(2, 0, S)
-        cast(3, 0, 512)
-        cast(3, 1, 208)
+        cast(3, 0, WIDTHS[3])
+        cast(3, 1, SHARE_PAIR3)
         x_codes = [
             keep.tile([P, S], U32, name="x_codes0", tag="raw3_0", align_bytes=64),
             keep.tile([P, S], U32, name="x_codes1", align_bytes=64),
         ]
         nc.vector.quantize_mx(out=x_codes[0][:].bitcast(FP8X4), scales=x_scales[0][:], in_=grouped0[:])
-        gather(3, 0, H)
-        gather(3, H, S)
+        gather(3, 0, HALF)
+        gather(3, HALF, S)
         w00 = interleave_w(0, 0, "wg00")
         grouped1 = keep.tile([P, S * 4], BF16, name="grouped1", align_bytes=64)
-        for lo in (0, H):
+        for lo in (0, HALF):
             nc.scalar.copy(
-                out=grouped1[:, 4 * lo : 4 * (lo + H)].bitcast(U32).rearrange("p (s u) -> p s u", u=2),
-                in_=picked[1][:, :, lo : lo + H].rearrange("p u s -> p s u"),
+                out=grouped1[:, 4 * lo : 4 * (lo + HALF)].bitcast(U32).rearrange("p (s u) -> p s u", u=2),
+                in_=picked[1][:, :, lo : lo + HALF].rearrange("p u s -> p s u"),
             )
         quantize_w(0, 0, w00)
         old = [keep.tile([P, S], F32, name="old0")]
@@ -127,24 +134,20 @@ def tile_picked_idxput_add_e_kernel(tc, xT, mem, w1, offs, slot, out):
         old.append(keep.tile([P, S], F32, name="old1", tag="wr01", align_bytes=64))
         nc.vector.tensor_copy(old[1][:], store[1][:].indirect(slot_sb[:]))
         w10 = interleave_w(1, 0, "wg10")
-        for z in range(2):
-            for h in range(2):
-                multiply(acc[0][h], 0, z, h * H, (h + 1) * H)
+        multiply(0)
         y0a = keep.tile([P, FIRST], F32, name="y0a")
         nc.scalar.copy(out=y0a[:], in_=acc[0][0][:, 0:FIRST])
         put(0, y0a, 0, FIRST)
         quantize_w(1, 0, w10)
         quantize_w(1, 1, interleave_w(1, 1, "wc0"))
         y0b = keep.tile([P, S - FIRST], F32, name="y0b", tag="wr11", align_bytes=64)
-        nc.scalar.copy(out=y0b[:, 0 : H - FIRST], in_=acc[0][0][:, FIRST:H])
-        nc.scalar.copy(out=y0b[:, H - FIRST : S - FIRST], in_=acc[0][1][:])
+        nc.scalar.copy(out=y0b[:, 0 : HALF - FIRST], in_=acc[0][0][:, FIRST:HALF])
+        nc.scalar.copy(out=y0b[:, HALF - FIRST : S - FIRST], in_=acc[0][1][:])
         put(0, y0b, FIRST, S)
         nc.sync.dma_start(out=out[0:P, :], in_=store[0][:])
-        for z in range(2):
-            for h in range(2):
-                multiply(acc[1][h], 1, z, h * H, (h + 1) * H)
+        multiply(1)
         y1 = keep.tile([P, S], F32, name="y1")
         for h in range(2):
-            nc.scalar.copy(out=y1[:, h * H : (h + 1) * H], in_=acc[1][h][:])
+            nc.scalar.copy(out=y1[:, h * HALF : (h + 1) * HALF], in_=acc[1][h][:])
         put(1, y1, 0, S)
         nc.sync.dma_start(out=out[P:N, :], in_=store[1][:])

@@ -19,7 +19,7 @@ HALF = S // 2
 WIDTHS = [T, T, T // 2, T // 2]
 SHARE_WHOLE = 336
 SHARE_PAIR2 = 224
-SHARE_PAIR3 = 208
+SHARE_PAIR3 = 160
 FIRST = 192
 
 
@@ -90,7 +90,7 @@ def tile_picked_idxput_add_e_kernel(tc, xT, mem, w1, offs, slot, out):
                         out=acc[b][h][:],
                         lhsT=w_codes[b][:, cols].bitcast(FP8X4),
                         lhsT_scale=w_scales[b][:, cols],
-                        rhs=x_codes[z][:, entries].bitcast(FP8X4),
+                        rhs=x_codes[z][h].bitcast(FP8X4),
                         rhs_scale=x_scales[z][:, entries],
                         start=(z == 0),
                         stop=(z == 1),
@@ -110,17 +110,18 @@ def tile_picked_idxput_add_e_kernel(tc, xT, mem, w1, offs, slot, out):
             in_=picked[0][:].bitcast(I32).rearrange("p u s -> p s u"),
         )
         gather(2, 0, S)
+        x_codes0 = [keep.tile([P, HALF], U32, name="x_codes00", tag="raw2_1", align_bytes=64)]
+        nc.vector.quantize_mx(out=x_codes0[0][:].bitcast(FP8X4), scales=x_scales[0][:, 0:HALF], in_=grouped0[:, 0 : 4 * HALF])
         cast(3, 0, WIDTHS[3])
         cast(3, 1, SHARE_PAIR3)
-        x_codes = [
-            keep.tile([P, S], U32, name="x_codes0", tag="raw3_0", align_bytes=64),
-            keep.tile([P, S], U32, name="x_codes1", align_bytes=64),
-        ]
-        nc.vector.quantize_mx(out=x_codes[0][:].bitcast(FP8X4), scales=x_scales[0][:], in_=grouped0[:])
+        x_codes0.append(keep.tile([P, HALF], U32, name="x_codes01", tag="raw3_0", align_bytes=64))
+        nc.vector.quantize_mx(out=x_codes0[1][:].bitcast(FP8X4), scales=x_scales[0][:, HALF:S], in_=grouped0[:, 4 * HALF : 4 * S])
+        x_codes1 = keep.tile([P, S], U32, name="x_codes1", align_bytes=64)
+        x_codes = [[x_codes0[h][:] for h in range(2)], [x_codes1[:, h * HALF : (h + 1) * HALF] for h in range(2)]]
         gather(3, 0, HALF)
         gather(3, HALF, S)
         w00 = interleave_w(0, 0, "wg00")
-        grouped1 = keep.tile([P, S * 4], BF16, name="grouped1", align_bytes=64)
+        grouped1 = keep.tile([P, S * 4], BF16, name="grouped1", tag="wr00", align_bytes=64)
         for lo in (0, HALF):
             nc.scalar.copy(
                 out=grouped1[:, 4 * lo : 4 * (lo + HALF)].bitcast(U32).rearrange("p (s u) -> p s u", u=2),
@@ -129,7 +130,7 @@ def tile_picked_idxput_add_e_kernel(tc, xT, mem, w1, offs, slot, out):
         quantize_w(0, 0, w00)
         old = [keep.tile([P, S], F32, name="old0")]
         nc.vector.tensor_copy(old[0][:], store[0][:].indirect(slot_sb[:]))
-        nc.vector.quantize_mx(out=x_codes[1][:].bitcast(FP8X4), scales=x_scales[1][:], in_=grouped1[:])
+        nc.vector.quantize_mx(out=x_codes1[:].bitcast(FP8X4), scales=x_scales[1][:], in_=grouped1[:])
         quantize_w(0, 1, interleave_w(0, 1, "wg01"))
         old.append(keep.tile([P, S], F32, name="old1", tag="wr01", align_bytes=64))
         nc.vector.tensor_copy(old[1][:], store[1][:].indirect(slot_sb[:]))

@@ -136,11 +136,11 @@ def tile_picked_idxput_add_e_kernel(tc, xT, mem, w1, offs, slot, out):
         nc.vector.tensor_copy(old[1][:], store[1][:].indirect(slot_sb[:]))
         w10 = interleave_w(1, 0, "wg10")
         multiply(0)
-        y0a = keep.tile([P, FIRST], F32, name="y0a")
+        quantize_w(1, 0, w10)
+        y0a = keep.tile([P, FIRST], F32, name="y0a", tag="wr10", align_bytes=64)
         nc.scalar.copy(out=y0a[:], in_=acc[0][0][:, 0:FIRST])
         put(0, y0a, 0, FIRST)
-        quantize_w(1, 0, w10)
-        quantize_w(1, 1, interleave_w(1, 1, "wc0"))
+        quantize_w(1, 1, interleave_w(1, 1, "wg10"))
         y0b = keep.tile([P, S - FIRST], F32, name="y0b", tag="wr11", align_bytes=64)
         nc.scalar.copy(out=y0b[:, 0 : HALF - FIRST], in_=acc[0][0][:, FIRST:HALF])
         nc.scalar.copy(out=y0b[:, HALF - FIRST : S - FIRST], in_=acc[0][1][:])

@@ -18,8 +18,8 @@ P = 128
 HALF = S // 2
 WIDTHS = [T, T, T // 2, T // 2]
 SHARE_WHOLE = 336
-SHARE_PAIR2 = 224
-SHARE_PAIR3 = 160
+SHARE_PAIR2 = 320
+SHARE_PAIR3 = 208
 FIRST = 192
 
 

@@ -7,20 +7,17 @@ FLOPS = 2 * K * N * S
 
 F32 = mybir.dt.float32
 BF16 = mybir.dt.bfloat16
-I32 = mybir.dt.int32
 U32 = mybir.dt.uint32
 U16 = mybir.dt.uint16
 U8 = mybir.dt.uint8
 FP8X4 = mybir.dt.float8_e4m3fn_x4
 ADD = mybir.AluOpType.add
+COPY = mybir.ActivationFunctionType.Copy
 
 P = 128
 HALF = S // 2
-WIDTHS = [T, T, T // 2, T // 2]
-SHARE_WHOLE = 336
-SHARE_PAIR2 = 320
-SHARE_PAIR3 = 208
-FIRST = 192
+FIRST = 128
+WEAVE_V = 352
 
 
 def tile_picked_idxput_add_e_kernel(tc, xT, mem, w1, offs, slot, out):
@@ -29,126 +26,115 @@ def tile_picked_idxput_add_e_kernel(tc, xT, mem, w1, offs, slot, out):
         keep = ctx.enter_context(tc.tile_pool(name="keep", bufs=1))
         psum = ctx.enter_context(tc.psum_pool(name="psum", bufs=1))
 
-        x_pairs = xT.rearrange("(z p u e) t -> z u p e t", z=2, p=P, u=2, e=2)
+        x_rows = xT.rearrange("(z p j) t -> z j p t", z=2, p=P, j=4)
         w_rows = w1.rearrange("(z p j) m -> z p j m", z=2, p=P, j=4)
 
         offs_sb = keep.tile([P, S // 16], U16, name="offs_sb")
         slot_sb = keep.tile([P, S // 16], U16, name="slot_sb")
-        raw = [[keep.tile([P, 2, WIDTHS[i]], F32, name="raw%d_%d" % (i, h), tag="raw%d_%d" % (i, h), align_bytes=64) for h in range(T // WIDTHS[i])] for i in range(4)]
-        w_raw = [[keep.tile([P, 4, P], F32, name="w_raw%d%d" % (b, z), tag="wr%d%d" % (b, z), align_bytes=64) for z in range(2)] for b in range(2)]
+        plane = [[keep.tile([P, T], F32, name="plane%d%d" % (z, j), align_bytes=64) for j in range(4)] for z in range(2)]
+        w_raw = [keep.tile([P, 4, N], F32, name="w_raw%d" % z, align_bytes=64) for z in range(2)]
         store = [keep.tile([P, U], F32, name="store%d" % b) for b in range(2)]
 
-        for i in range(4):
-            for h in range(T // WIDTHS[i]):
-                nc.sync.dma_start(out=raw[i][h][:], in_=x_pairs[i // 2, i % 2][:, :, h * WIDTHS[i] : (h + 1) * WIDTHS[i]])
-            if i == 0:
-                nc.sync.dma_start(offs_sb[:], offs)
         for z in range(2):
-            nc.sync.dma_start(out=w_raw[0][z][:], in_=w_rows[z][:, :, 0:P])
-            if z == 0:
-                nc.sync.dma_start(slot_sb[:], slot)
-            nc.sync.dma_start(out=store[z][:], in_=mem[z * P : (z + 1) * P, :])
+            for j in range(4):
+                nc.sync.dma_start(out=plane[z][j][:], in_=x_rows[z, j])
+                if z == 0 and j == 0:
+                    nc.sync.dma_start(offs_sb[:], offs)
         for z in range(2):
-            nc.sync.dma_start(out=w_raw[1][z][:], in_=w_rows[z][:, :, P:N])
+            nc.sync.dma_start(out=w_raw[z][:], in_=w_rows[z])
+        nc.sync.dma_start(slot_sb[:], slot)
+        for b in range(2):
+            nc.sync.dma_start(out=store[b][:], in_=mem[b * P : (b + 1) * P, :])
 
-        pairs = [keep.tile([P, T, 2], BF16, name="pairs%d" % i, align_bytes=64) for i in range(4)]
-        picked = [keep.tile([P, 2, S], U32, name="picked%d" % z, align_bytes=64) for z in range(2)]
+        picked = [keep.tile([P, 4, S], BF16, name="picked%d" % z, align_bytes=64) for z in range(2)]
+        grouped = [keep.tile([P, S * 4], BF16, name="grouped%d" % z, align_bytes=64) for z in range(2)]
+        x_codes = [keep.tile([P, S], U32, name="x_codes%d" % z, align_bytes=64) for z in range(2)]
         x_scales = [keep.tile([P, S], U8, name="x_scales%d" % z, align_bytes=64) for z in range(2)]
-        w_codes = [keep.tile([P, 2 * P], U32, name="w_codes%d" % b, tag="wc%d" % b, align_bytes=64) for b in range(2)]
-        w_scales = [keep.tile([P, 2 * P], U8, name="w_scales%d" % b, align_bytes=64) for b in range(2)]
+        w_grouped = [[keep.tile([P, 4 * P], BF16, name="w_grouped%d%d" % (b, z), tag="wg%d%d" % (b, z), align_bytes=64) for z in range(2)] for b in range(2)]
+        w_codes = {}
+        w_scales = [[keep.tile([P, P], U8, name="w_scales%d%d" % (b, z), align_bytes=64) for z in range(2)] for b in range(2)]
         acc = [[psum.tile([P, HALF], F32, name="acc%d%d" % (b, h)) for h in range(2)] for b in range(2)]
+        old0 = [keep.tile([P, HALF], F32, name="old0%d" % h, tag="old0%d" % h) for h in range(2)]
+        old1 = keep.tile([P, S], F32, name="old1")
 
-        def cast(i, h, share):
-            width = WIDTHS[i]
-            t0 = h * width
-            nc.scalar.copy(out=pairs[i][:, t0 : t0 + share, :], in_=raw[i][h][:, :, 0:share].rearrange("p e t -> p t e"))
-            if share < width:
-                nc.vector.tensor_copy(out=pairs[i][:, t0 + share : t0 + width, :], in_=raw[i][h][:, :, share:width].rearrange("p e t -> p t e"))
+        def gather_v(dst, window, lst, lo, hi):
+            nc.vector.tensor_copy(dst, window[:].indirect(lst[:, lo // 16 : hi // 16]))
 
-        def gather(i, lo, hi):
-            window = pairs[i][:].rearrange("p t e -> p (t e)").bitcast(U32)
-            nc.vector.tensor_copy(picked[i // 2][:, i % 2, lo:hi], window.indirect(offs_sb[:, lo // 16 : hi // 16]))
+        def gather_s(dst, window, lst, lo, hi):
+            nc.scalar.activation(dst, window[:].indirect(lst[:, lo // 16 : hi // 16]), COPY)
 
-        def interleave_w(b, z, tag):
-            grouped = keep.tile([P, 4 * P], BF16, name="w_grouped%d%d" % (b, z), tag=tag, align_bytes=64)
-            nc.scalar.copy(
-                out=grouped[:].rearrange("p (c i j) -> p c j i", i=4, j=4),
-                in_=w_raw[b][z][:].rearrange("p j (c i) -> p c j i", i=4),
+        def weave(copy, z, lo, hi):
+            copy(
+                out=grouped[z][:, 4 * lo : 4 * hi].rearrange("p (c i j) -> p c j i", i=4, j=4),
+                in_=picked[z][:, :, lo:hi].rearrange("p j (c i) -> p c j i", i=4),
             )
-            return grouped
 
-        def quantize_w(b, z, grouped):
-            cols = slice(z * P, (z + 1) * P)
-            nc.vector.quantize_mx(out=w_codes[b][:, cols].bitcast(FP8X4), scales=w_scales[b][:, cols], in_=grouped[:])
-
-        def multiply(b):
-            for z in range(2):
-                cols = slice(z * P, (z + 1) * P)
-                for h in range(2):
-                    entries = slice(h * HALF, (h + 1) * HALF)
-                    nc.tensor.matmul_mx(
-                        out=acc[b][h][:],
-                        lhsT=w_codes[b][:, cols].bitcast(FP8X4),
-                        lhsT_scale=w_scales[b][:, cols],
-                        rhs=x_codes[z][h].bitcast(FP8X4),
-                        rhs_scale=x_scales[z][:, entries],
-                        start=(z == 0),
-                        stop=(z == 1),
-                    )
-
-        def put(b, y, lo, hi):
-            nc.vector.tensor_tensor(store[b][:].indirect(slot_sb[:, lo // 16 : hi // 16]), old[b][:, lo:hi], y[:], ADD)
-
-        for i in range(2):
-            cast(i, 0, SHARE_WHOLE)
-            gather(i, 0, S)
-        cast(2, 0, WIDTHS[2])
-        cast(2, 1, SHARE_PAIR2)
-        grouped0 = keep.tile([P, S * 4], BF16, name="grouped0", tag="raw2_0", align_bytes=64)
-        nc.vector.tensor_copy(
-            out=grouped0[:].bitcast(I32).rearrange("p (s u) -> p s u", u=2),
-            in_=picked[0][:].bitcast(I32).rearrange("p u s -> p s u"),
-        )
-        gather(2, 0, S)
-        x_codes0 = [keep.tile([P, HALF], U32, name="x_codes00", tag="raw2_1", align_bytes=64)]
-        nc.vector.quantize_mx(out=x_codes0[0][:].bitcast(FP8X4), scales=x_scales[0][:, 0:HALF], in_=grouped0[:, 0 : 4 * HALF])
-        cast(3, 0, WIDTHS[3])
-        cast(3, 1, SHARE_PAIR3)
-        x_codes0.append(keep.tile([P, HALF], U32, name="x_codes01", tag="raw3_0", align_bytes=64))
-        nc.vector.quantize_mx(out=x_codes0[1][:].bitcast(FP8X4), scales=x_scales[0][:, HALF:S], in_=grouped0[:, 4 * HALF : 4 * S])
-        x_codes1 = keep.tile([P, S], U32, name="x_codes1", align_bytes=64)
-        x_codes = [[x_codes0[h][:] for h in range(2)], [x_codes1[:, h * HALF : (h + 1) * HALF] for h in range(2)]]
-        gather(3, 0, HALF)
-        gather(3, HALF, S)
-        w00 = interleave_w(0, 0, "wg00")
-        grouped1 = keep.tile([P, S * 4], BF16, name="grouped1", tag="wr00", align_bytes=64)
-        for lo in (0, HALF):
-            nc.scalar.copy(
-                out=grouped1[:, 4 * lo : 4 * (lo + HALF)].bitcast(U32).rearrange("p (s u) -> p s u", u=2),
-                in_=picked[1][:, :, lo : lo + HALF].rearrange("p u s -> p s u"),
+        def interleave_w(copy, b, z):
+            copy(
+                out=w_grouped[b][z][:].rearrange("p (c i j) -> p c j i", i=4, j=4),
+                in_=w_raw[z][:, :, b * P : (b + 1) * P].rearrange("p j (c i) -> p c j i", i=4),
             )
-        quantize_w(0, 0, w00)
-        old = [keep.tile([P, S], F32, name="old0")]
-        nc.vector.tensor_copy(old[0][:], store[0][:].indirect(slot_sb[:]))
-        nc.vector.quantize_mx(out=x_codes1[:].bitcast(FP8X4), scales=x_scales[1][:], in_=grouped1[:])
-        quantize_w(0, 1, interleave_w(0, 1, "wg01"))
-        old.append(keep.tile([P, S], F32, name="old1", tag="wr01", align_bytes=64))
-        nc.vector.tensor_copy(old[1][:], store[1][:].indirect(slot_sb[:]))
-        w10 = interleave_w(1, 0, "wg10")
-        multiply(0)
-        quantize_w(1, 0, w10)
-        y0a = keep.tile([P, FIRST], F32, name="y0a", tag="wr10", align_bytes=64)
-        nc.scalar.copy(out=y0a[:], in_=acc[0][0][:, 0:FIRST])
-        put(0, y0a, 0, FIRST)
-        quantize_w(1, 1, interleave_w(1, 1, "wg10"))
-        y0b = keep.tile([P, S - FIRST], F32, name="y0b", tag="wr11", align_bytes=64)
-        nc.scalar.copy(out=y0b[:, 0 : HALF - FIRST], in_=acc[0][0][:, FIRST:HALF])
-        nc.scalar.copy(out=y0b[:, HALF - FIRST : S - FIRST], in_=acc[0][1][:])
-        put(0, y0b, FIRST, S)
-        nc.sync.dma_start(out=out[0:P, :], in_=store[0][:])
-        multiply(1)
-        y1 = keep.tile([P, S], F32, name="y1")
+
+        def quantize_x(z):
+            nc.vector.quantize_mx(out=x_codes[z][:].bitcast(FP8X4), scales=x_scales[z][:], in_=grouped[z][:])
+
+        def quantize_w(b, z, tag):
+            w_codes[b, z] = keep.tile([P, P], U32, name="w_codes%d%d" % (b, z), tag=tag, align_bytes=64)
+            nc.vector.quantize_mx(out=w_codes[b, z][:].bitcast(FP8X4), scales=w_scales[b][z][:], in_=w_grouped[b][z][:])
+
+        def multiply(b, z):
+            for h in range(2):
+                entries = slice(h * HALF, (h + 1) * HALF)
+                nc.tensor.matmul_mx(
+                    out=acc[b][h][:],
+                    lhsT=w_codes[b, z][:].bitcast(FP8X4),
+                    lhsT_scale=w_scales[b][z][:],
+                    rhs=x_codes[z][:, entries].bitcast(FP8X4),
+                    rhs_scale=x_scales[z][:, entries],
+                    start=(z == 0),
+                    stop=(z == 1),
+                )
+
+        gather_s(picked[0][:, 0, :], plane[0][0], offs_sb, 0, S)
+        gather_v(picked[0][:, 1, :], plane[0][1], offs_sb, 0, S)
+        gather_v(picked[0][:, 2, :], plane[0][2], offs_sb, 0, S)
+        gather_v(picked[0][:, 3, 0:HALF], plane[0][3], offs_sb, 0, HALF)
+        gather_s(picked[0][:, 3, HALF:S], plane[0][3], offs_sb, HALF, S)
+        weave(nc.vector.tensor_copy, 0, 0, S)
+        gather_s(picked[1][:, 0, :], plane[1][0], offs_sb, 0, S)
+        quantize_x(0)
+        gather_s(picked[1][:, 1, :], plane[1][1], offs_sb, 0, S)
+        gather_v(picked[1][:, 2, :], plane[1][2], offs_sb, 0, S)
+        gather_v(picked[1][:, 3, 0:HALF], plane[1][3], offs_sb, 0, HALF)
+        gather_s(picked[1][:, 3, HALF:S], plane[1][3], offs_sb, HALF, S)
+        weave(nc.vector.tensor_copy, 1, 0, WEAVE_V)
+        weave(nc.scalar.copy, 1, WEAVE_V, S)
+        interleave_w(nc.vector.tensor_copy, 0, 0)
+        interleave_w(nc.scalar.copy, 1, 0)
+        quantize_x(1)
+        quantize_w(0, 0, "wc00")
+        multiply(0, 0)
+        interleave_w(nc.scalar.copy, 0, 1)
+        quantize_w(0, 1, "wc01")
+        multiply(0, 1)
+        interleave_w(nc.scalar.copy, 1, 1)
+        quantize_w(1, 0, "wg01")
+        gather_v(old0[0][:], store[0], slot_sb, 0, HALF)
+        gather_s(old0[1][:], store[0], slot_sb, HALF, S)
+        multiply(1, 0)
+        quantize_w(1, 1, "wc11")
+        multiply(1, 1)
+        new0a = keep.tile([P, FIRST], F32, name="new0a")
+        nc.vector.tensor_tensor(new0a[:], acc[0][0][:, 0:FIRST], old0[0][:, 0:FIRST], ADD)
+        nc.scalar.activation(store[0][:].indirect(slot_sb[:, 0 : FIRST // 16]), new0a[:], COPY)
+        new0b = keep.tile([P, S - FIRST], F32, name="new0b")
+        nc.vector.tensor_tensor(new0b[:, 0 : HALF - FIRST], acc[0][0][:, FIRST:HALF], old0[0][:, FIRST:HALF], ADD)
+        nc.vector.tensor_tensor(new0b[:, HALF - FIRST : S - FIRST], acc[0][1][:], old0[1][:], ADD)
+        gather_v(old1[:], store[1], slot_sb, 0, S)
+        y1 = keep.tile([P, S], F32, name="y1", tag="old01")
         for h in range(2):
             nc.scalar.copy(out=y1[:, h * HALF : (h + 1) * HALF], in_=acc[1][h][:])
-        put(1, y1, 0, S)
+        nc.scalar.activation(store[0][:].indirect(slot_sb[:, FIRST // 16 : S // 16]), new0b[:], COPY)
+        nc.sync.dma_start(out=out[0:P, :], in_=store[0][:])
+        nc.vector.tensor_tensor(store[1][:].indirect(slot_sb[:]), old1[:], y1[:], ADD)
         nc.sync.dma_start(out=out[P:N, :], in_=store[1][:])

@@ -17,6 +17,9 @@ COPY = mybir.ActivationFunctionType.Copy
 P = 128
 HALF = S // 2
 FIRST = 128
+OLD_S = 352
+GROUPS = [(0, 1), (1, 3), (3, 4)]
+START_V = 384
 WEAVE_V = 352
 
 
@@ -26,19 +29,20 @@ def tile_picked_idxput_add_e_kernel(tc, xT, mem, w1, offs, slot, out):
         keep = ctx.enter_context(tc.tile_pool(name="keep", bufs=1))
         psum = ctx.enter_context(tc.psum_pool(name="psum", bufs=1))
 
-        x_rows = xT.rearrange("(z p j) t -> z j p t", z=2, p=P, j=4)
+        x_rows = xT.rearrange("(z p j) t -> z p j t", z=2, p=P, j=4)
         w_rows = w1.rearrange("(z p j) m -> z p j m", z=2, p=P, j=4)
 
         offs_sb = keep.tile([P, S // 16], U16, name="offs_sb")
         slot_sb = keep.tile([P, S // 16], U16, name="slot_sb")
-        plane = [[keep.tile([P, T], F32, name="plane%d%d" % (z, j), align_bytes=64) for j in range(4)] for z in range(2)]
-        w_raw = [keep.tile([P, 4, N], F32, name="w_raw%d" % z, align_bytes=64) for z in range(2)]
+        loads = [[keep.tile([P, j1 - j0, T], F32, name="x%d%d" % (z, j0), align_bytes=64) for j0, j1 in GROUPS] for z in range(2)]
+        plane = [[loads[z][g][:, j - j0, :] for g, (j0, j1) in enumerate(GROUPS) for j in range(j0, j1)] for z in range(2)]
+        w_raw = [keep.tile([P, 4, N], F32, name="w_raw%d" % z, tag="w_raw%d" % z, align_bytes=64) for z in range(2)]
         store = [keep.tile([P, U], F32, name="store%d" % b) for b in range(2)]
 
         for z in range(2):
-            for j in range(4):
-                nc.sync.dma_start(out=plane[z][j][:], in_=x_rows[z, j])
-                if z == 0 and j == 0:
+            for g, (j0, j1) in enumerate(GROUPS):
+                nc.sync.dma_start(out=loads[z][g][:], in_=x_rows[z][:, j0:j1, :])
+                if z == 0 and g == 0:
                     nc.sync.dma_start(offs_sb[:], offs)
         for z in range(2):
             nc.sync.dma_start(out=w_raw[z][:], in_=w_rows[z])
@@ -46,22 +50,22 @@ def tile_picked_idxput_add_e_kernel(tc, xT, mem, w1, offs, slot, out):
         for b in range(2):
             nc.sync.dma_start(out=store[b][:], in_=mem[b * P : (b + 1) * P, :])
 
-        picked = [keep.tile([P, 4, S], BF16, name="picked%d" % z, align_bytes=64) for z in range(2)]
+        picked = [keep.tile([P, 4, S], F32, name="picked%d" % z, align_bytes=64) for z in range(2)]
         grouped = [keep.tile([P, S * 4], BF16, name="grouped%d" % z, align_bytes=64) for z in range(2)]
         x_codes = [keep.tile([P, S], U32, name="x_codes%d" % z, align_bytes=64) for z in range(2)]
         x_scales = [keep.tile([P, S], U8, name="x_scales%d" % z, align_bytes=64) for z in range(2)]
-        w_grouped = [[keep.tile([P, 4 * P], BF16, name="w_grouped%d%d" % (b, z), tag="wg%d%d" % (b, z), align_bytes=64) for z in range(2)] for b in range(2)]
-        w_codes = {}
-        w_scales = [[keep.tile([P, P], U8, name="w_scales%d%d" % (b, z), align_bytes=64) for z in range(2)] for b in range(2)]
+        w_grouped = [keep.tile([P, 2, 4 * P], BF16, name="w_grouped%d" % b, align_bytes=64) for b in range(2)]
+        w_codes = [keep.tile([P, 2 * P], U32, name="w_codes0", align_bytes=64)]
+        w_scales = [keep.tile([P, 2 * P], U8, name="w_scales%d" % b, align_bytes=64) for b in range(2)]
         acc = [[psum.tile([P, HALF], F32, name="acc%d%d" % (b, h)) for h in range(2)] for b in range(2)]
-        old0 = [keep.tile([P, HALF], F32, name="old0%d" % h, tag="old0%d" % h) for h in range(2)]
+        old0 = keep.tile([P, S], F32, name="old0", tag="old0")
         old1 = keep.tile([P, S], F32, name="old1")
 
         def gather_v(dst, window, lst, lo, hi):
-            nc.vector.tensor_copy(dst, window[:].indirect(lst[:, lo // 16 : hi // 16]))
+            nc.vector.tensor_copy(dst, window.indirect(lst[:, lo // 16 : hi // 16]))
 
         def gather_s(dst, window, lst, lo, hi):
-            nc.scalar.activation(dst, window[:].indirect(lst[:, lo // 16 : hi // 16]), COPY)
+            nc.scalar.activation(dst, window.indirect(lst[:, lo // 16 : hi // 16]), COPY)
 
         def weave(copy, z, lo, hi):
             copy(
@@ -71,40 +75,41 @@ def tile_picked_idxput_add_e_kernel(tc, xT, mem, w1, offs, slot, out):
 
         def interleave_w(copy, b, z):
             copy(
-                out=w_grouped[b][z][:].rearrange("p (c i j) -> p c j i", i=4, j=4),
+                out=w_grouped[b][:, z, :].rearrange("p (c i j) -> p c j i", i=4, j=4),
                 in_=w_raw[z][:, :, b * P : (b + 1) * P].rearrange("p j (c i) -> p c j i", i=4),
             )
 
         def quantize_x(z):
             nc.vector.quantize_mx(out=x_codes[z][:].bitcast(FP8X4), scales=x_scales[z][:], in_=grouped[z][:])
 
-        def quantize_w(b, z, tag):
-            w_codes[b, z] = keep.tile([P, P], U32, name="w_codes%d%d" % (b, z), tag=tag, align_bytes=64)
-            nc.vector.quantize_mx(out=w_codes[b, z][:].bitcast(FP8X4), scales=w_scales[b][z][:], in_=w_grouped[b][z][:])
+        def quantize_w(b, z0, z1):
+            cols = slice(z0 * P, z1 * P)
+            nc.vector.quantize_mx(out=w_codes[b][:, cols].bitcast(FP8X4), scales=w_scales[b][:, cols], in_=w_grouped[b][:, z0:z1, :].rearrange("p z c -> p (z c)"))
 
         def multiply(b, z):
             for h in range(2):
                 entries = slice(h * HALF, (h + 1) * HALF)
                 nc.tensor.matmul_mx(
                     out=acc[b][h][:],
-                    lhsT=w_codes[b, z][:].bitcast(FP8X4),
-                    lhsT_scale=w_scales[b][z][:],
+                    lhsT=w_codes[b][:, z * P : (z + 1) * P].bitcast(FP8X4),
+                    lhsT_scale=w_scales[b][:, z * P : (z + 1) * P],
                     rhs=x_codes[z][:, entries].bitcast(FP8X4),
                     rhs_scale=x_scales[z][:, entries],
                     start=(z == 0),
                     stop=(z == 1),
                 )
 
-        gather_s(picked[0][:, 0, :], plane[0][0], offs_sb, 0, S)
+        gather_v(picked[0][:, 0, 0:START_V], plane[0][0], offs_sb, 0, START_V)
+        gather_s(picked[0][:, 0, START_V:S], plane[0][0], offs_sb, START_V, S)
         gather_v(picked[0][:, 1, :], plane[0][1], offs_sb, 0, S)
-        gather_v(picked[0][:, 2, :], plane[0][2], offs_sb, 0, S)
+        gather_s(picked[0][:, 2, :], plane[0][2], offs_sb, 0, S)
         gather_v(picked[0][:, 3, 0:HALF], plane[0][3], offs_sb, 0, HALF)
         gather_s(picked[0][:, 3, HALF:S], plane[0][3], offs_sb, HALF, S)
         weave(nc.vector.tensor_copy, 0, 0, S)
         gather_s(picked[1][:, 0, :], plane[1][0], offs_sb, 0, S)
         quantize_x(0)
-        gather_s(picked[1][:, 1, :], plane[1][1], offs_sb, 0, S)
-        gather_v(picked[1][:, 2, :], plane[1][2], offs_sb, 0, S)
+        gather_v(picked[1][:, 1, :], plane[1][1], offs_sb, 0, S)
+        gather_s(picked[1][:, 2, :], plane[1][2], offs_sb, 0, S)
         gather_v(picked[1][:, 3, 0:HALF], plane[1][3], offs_sb, 0, HALF)
         gather_s(picked[1][:, 3, HALF:S], plane[1][3], offs_sb, HALF, S)
         weave(nc.vector.tensor_copy, 1, 0, WEAVE_V)
@@ -112,26 +117,27 @@ def tile_picked_idxput_add_e_kernel(tc, xT, mem, w1, offs, slot, out):
         interleave_w(nc.vector.tensor_copy, 0, 0)
         interleave_w(nc.scalar.copy, 1, 0)
         quantize_x(1)
-        quantize_w(0, 0, "wc00")
+        quantize_w(0, 0, 1)
         multiply(0, 0)
         interleave_w(nc.scalar.copy, 0, 1)
-        quantize_w(0, 1, "wc01")
+        interleave_w(nc.vector.tensor_copy, 1, 1)
+        quantize_w(0, 1, 2)
         multiply(0, 1)
-        interleave_w(nc.scalar.copy, 1, 1)
-        quantize_w(1, 0, "wg01")
-        gather_v(old0[0][:], store[0], slot_sb, 0, HALF)
-        gather_s(old0[1][:], store[0], slot_sb, HALF, S)
+        w_codes.append(keep.tile([P, 2 * P], U32, name="w_codes1", tag="w_raw1", align_bytes=64))
+        quantize_w(1, 0, 2)
+        gather_s(old0[:, 0:FIRST], store[0][:], slot_sb, 0, FIRST)
+        gather_s(old0[:, FIRST:OLD_S], store[0][:], slot_sb, FIRST, OLD_S)
+        gather_v(old0[:, OLD_S:S], store[0][:], slot_sb, OLD_S, S)
         multiply(1, 0)
-        quantize_w(1, 1, "wc11")
         multiply(1, 1)
         new0a = keep.tile([P, FIRST], F32, name="new0a")
-        nc.vector.tensor_tensor(new0a[:], acc[0][0][:, 0:FIRST], old0[0][:, 0:FIRST], ADD)
+        nc.vector.tensor_tensor(new0a[:], acc[0][0][:, 0:FIRST], old0[:, 0:FIRST], ADD)
         nc.scalar.activation(store[0][:].indirect(slot_sb[:, 0 : FIRST // 16]), new0a[:], COPY)
         new0b = keep.tile([P, S - FIRST], F32, name="new0b")
-        nc.vector.tensor_tensor(new0b[:, 0 : HALF - FIRST], acc[0][0][:, FIRST:HALF], old0[0][:, FIRST:HALF], ADD)
-        nc.vector.tensor_tensor(new0b[:, HALF - FIRST : S - FIRST], acc[0][1][:], old0[1][:], ADD)
-        gather_v(old1[:], store[1], slot_sb, 0, S)
-        y1 = keep.tile([P, S], F32, name="y1", tag="old01")
+        nc.vector.tensor_tensor(new0b[:, 0 : HALF - FIRST], acc[0][0][:, FIRST:HALF], old0[:, FIRST:HALF], ADD)
+        nc.vector.tensor_tensor(new0b[:, HALF - FIRST : S - FIRST], acc[0][1][:], old0[:, HALF:S], ADD)
+        gather_v(old1[:], store[1][:], slot_sb, 0, S)
+        y1 = keep.tile([P, S], F32, name="y1", tag="old0")
         for h in range(2):
             nc.scalar.copy(out=y1[:, h * HALF : (h + 1) * HALF], in_=acc[1][h][:])
         nc.scalar.activation(store[0][:].indirect(slot_sb[:, FIRST // 16 : S // 16]), new0b[:], COPY)

@@ -17,10 +17,12 @@ COPY = mybir.ActivationFunctionType.Copy
 P = 128
 HALF = S // 2
 FIRST = 128
-OLD_S = 352
-GROUPS = [(0, 1), (1, 3), (3, 4)]
+OLD_S = 320
+GROUPS = [[(0, 1), (1, 3), (3, 4)], [(0, 2), (2, 3), (3, 4)]]
 START_V = 384
-WEAVE_V = 352
+WEAVE0_V = 320
+THIRD_V = 160
+WEAVE_V = 320
 
 
 def tile_picked_idxput_add_e_kernel(tc, xT, mem, w1, offs, slot, out):
@@ -34,13 +36,13 @@ def tile_picked_idxput_add_e_kernel(tc, xT, mem, w1, offs, slot, out):
 
         offs_sb = keep.tile([P, S // 16], U16, name="offs_sb")
         slot_sb = keep.tile([P, S // 16], U16, name="slot_sb")
-        loads = [[keep.tile([P, j1 - j0, T], F32, name="x%d%d" % (z, j0), align_bytes=64) for j0, j1 in GROUPS] for z in range(2)]
-        plane = [[loads[z][g][:, j - j0, :] for g, (j0, j1) in enumerate(GROUPS) for j in range(j0, j1)] for z in range(2)]
+        loads = [[keep.tile([P, j1 - j0, T], F32, name="x%d%d" % (z, j0), align_bytes=64) for j0, j1 in GROUPS[z]] for z in range(2)]
+        plane = [[loads[z][g][:, j - j0, :] for g, (j0, j1) in enumerate(GROUPS[z]) for j in range(j0, j1)] for z in range(2)]
         w_raw = [keep.tile([P, 4, N], F32, name="w_raw%d" % z, tag="w_raw%d" % z, align_bytes=64) for z in range(2)]
         store = [keep.tile([P, U], F32, name="store%d" % b) for b in range(2)]
 
         for z in range(2):
-            for g, (j0, j1) in enumerate(GROUPS):
+            for g, (j0, j1) in enumerate(GROUPS[z]):
                 nc.sync.dma_start(out=loads[z][g][:], in_=x_rows[z][:, j0:j1, :])
                 if z == 0 and g == 0:
                     nc.sync.dma_start(offs_sb[:], offs)
@@ -105,11 +107,13 @@ def tile_picked_idxput_add_e_kernel(tc, xT, mem, w1, offs, slot, out):
         gather_s(picked[0][:, 2, :], plane[0][2], offs_sb, 0, S)
         gather_v(picked[0][:, 3, 0:HALF], plane[0][3], offs_sb, 0, HALF)
         gather_s(picked[0][:, 3, HALF:S], plane[0][3], offs_sb, HALF, S)
-        weave(nc.vector.tensor_copy, 0, 0, S)
+        weave(nc.vector.tensor_copy, 0, 0, WEAVE0_V)
+        weave(nc.scalar.copy, 0, WEAVE0_V, S)
         gather_s(picked[1][:, 0, :], plane[1][0], offs_sb, 0, S)
         quantize_x(0)
         gather_v(picked[1][:, 1, :], plane[1][1], offs_sb, 0, S)
-        gather_s(picked[1][:, 2, :], plane[1][2], offs_sb, 0, S)
+        gather_v(picked[1][:, 2, 0:THIRD_V], plane[1][2], offs_sb, 0, THIRD_V)
+        gather_s(picked[1][:, 2, THIRD_V:S], plane[1][2], offs_sb, THIRD_V, S)
         gather_v(picked[1][:, 3, 0:HALF], plane[1][3], offs_sb, 0, HALF)
         gather_s(picked[1][:, 3, HALF:S], plane[1][3], offs_sb, HALF, S)
         weave(nc.vector.tensor_copy, 1, 0, WEAVE_V)

@@ -16,13 +16,11 @@ COPY = mybir.ActivationFunctionType.Copy
 
 P = 128
 HALF = S // 2
-FIRST = 128
-OLD_S = 320
 GROUPS = [[(0, 1), (1, 3), (3, 4)], [(0, 2), (2, 3), (3, 4)]]
-START_V = 384
-WEAVE0_V = 320
-THIRD_V = 160
-WEAVE_V = 320
+HELP = 128
+WEAVE_V = [128, 160]
+FIRST = 128
+OLD_V = 224
 
 
 def tile_picked_idxput_add_e_kernel(tc, xT, mem, w1, offs, slot, out):
@@ -36,9 +34,9 @@ def tile_picked_idxput_add_e_kernel(tc, xT, mem, w1, offs, slot, out):
 
         offs_sb = keep.tile([P, S // 16], U16, name="offs_sb")
         slot_sb = keep.tile([P, S // 16], U16, name="slot_sb")
-        loads = [[keep.tile([P, j1 - j0, T], F32, name="x%d%d" % (z, j0), align_bytes=64) for j0, j1 in GROUPS[z]] for z in range(2)]
+        loads = [[keep.tile([P, j1 - j0, T], F32, name="x%d%d" % (z, j0), tag="x%d%d" % (z, j0), align_bytes=64) for j0, j1 in GROUPS[z]] for z in range(2)]
         plane = [[loads[z][g][:, j - j0, :] for g, (j0, j1) in enumerate(GROUPS[z]) for j in range(j0, j1)] for z in range(2)]
-        w_raw = [keep.tile([P, 4, N], F32, name="w_raw%d" % z, tag="w_raw%d" % z, align_bytes=64) for z in range(2)]
+        w_raw = [keep.tile([P, 4, N], F32, name="w_raw%d" % z, align_bytes=64) for z in range(2)]
         store = [keep.tile([P, U], F32, name="store%d" % b) for b in range(2)]
 
         for z in range(2):
@@ -52,12 +50,12 @@ def tile_picked_idxput_add_e_kernel(tc, xT, mem, w1, offs, slot, out):
         for b in range(2):
             nc.sync.dma_start(out=store[b][:], in_=mem[b * P : (b + 1) * P, :])
 
-        picked = [keep.tile([P, 4, S], F32, name="picked%d" % z, align_bytes=64) for z in range(2)]
+        picked = [keep.tile([P, 4, HALF], F32, name="picked%d" % z, align_bytes=64) for z in range(2)]
         grouped = [keep.tile([P, S * 4], BF16, name="grouped%d" % z, align_bytes=64) for z in range(2)]
-        x_codes = [keep.tile([P, S], U32, name="x_codes%d" % z, align_bytes=64) for z in range(2)]
+        x_codes = []
         x_scales = [keep.tile([P, S], U8, name="x_scales%d" % z, align_bytes=64) for z in range(2)]
-        w_grouped = [keep.tile([P, 2, 4 * P], BF16, name="w_grouped%d" % b, align_bytes=64) for b in range(2)]
-        w_codes = [keep.tile([P, 2 * P], U32, name="w_codes0", align_bytes=64)]
+        w_grouped = [keep.tile([P, 2 * 4 * P], BF16, name="w_grouped%d" % b, align_bytes=64) for b in range(2)]
+        w_codes = [keep.tile([P, 2 * P], U32, name="w_codes%d" % b, align_bytes=64) for b in range(2)]
         w_scales = [keep.tile([P, 2 * P], U8, name="w_scales%d" % b, align_bytes=64) for b in range(2)]
         acc = [[psum.tile([P, HALF], F32, name="acc%d%d" % (b, h)) for h in range(2)] for b in range(2)]
         old0 = keep.tile([P, S], F32, name="old0", tag="old0")
@@ -69,71 +67,67 @@ def tile_picked_idxput_add_e_kernel(tc, xT, mem, w1, offs, slot, out):
         def gather_s(dst, window, lst, lo, hi):
             nc.scalar.activation(dst, window.indirect(lst[:, lo // 16 : hi // 16]), COPY)
 
-        def weave(copy, z, lo, hi):
-            copy(
-                out=grouped[z][:, 4 * lo : 4 * hi].rearrange("p (c i j) -> p c j i", i=4, j=4),
-                in_=picked[z][:, :, lo:hi].rearrange("p j (c i) -> p c j i", i=4),
-            )
+        def interleave(copy, dst, src):
+            copy(out=dst.rearrange("p (c i j) -> p c j i", i=4, j=4), in_=src.rearrange("p j (c i) -> p c j i", i=4))
 
-        def interleave_w(copy, b, z):
-            copy(
-                out=w_grouped[b][:, z, :].rearrange("p (c i j) -> p c j i", i=4, j=4),
-                in_=w_raw[z][:, :, b * P : (b + 1) * P].rearrange("p j (c i) -> p c j i", i=4),
-            )
+        def quantize_x(z, h):
+            lo, hi = h * HALF, (h + 1) * HALF
+            nc.vector.quantize_mx(out=x_codes[z][h][:].bitcast(FP8X4), scales=x_scales[z][:, lo:hi], in_=grouped[z][:, 4 * lo : 4 * hi])
 
-        def quantize_x(z):
-            nc.vector.quantize_mx(out=x_codes[z][:].bitcast(FP8X4), scales=x_scales[z][:], in_=grouped[z][:])
+        def interleave_w(copy, b, z, lo=0, hi=P):
+            interleave(copy, w_grouped[b][:, 4 * (z * P + lo) : 4 * (z * P + hi)], w_raw[z][:, :, b * P + lo : b * P + hi])
 
         def quantize_w(b, z0, z1):
             cols = slice(z0 * P, z1 * P)
-            nc.vector.quantize_mx(out=w_codes[b][:, cols].bitcast(FP8X4), scales=w_scales[b][:, cols], in_=w_grouped[b][:, z0:z1, :].rearrange("p z c -> p (z c)"))
+            nc.vector.quantize_mx(out=w_codes[b][:, cols].bitcast(FP8X4), scales=w_scales[b][:, cols], in_=w_grouped[b][:, 4 * z0 * P : 4 * z1 * P])
 
-        def multiply(b, z):
-            for h in range(2):
-                entries = slice(h * HALF, (h + 1) * HALF)
-                nc.tensor.matmul_mx(
-                    out=acc[b][h][:],
-                    lhsT=w_codes[b][:, z * P : (z + 1) * P].bitcast(FP8X4),
-                    lhsT_scale=w_scales[b][:, z * P : (z + 1) * P],
-                    rhs=x_codes[z][:, entries].bitcast(FP8X4),
-                    rhs_scale=x_scales[z][:, entries],
-                    start=(z == 0),
-                    stop=(z == 1),
-                )
+        def multiply(b, z, h):
+            entries = slice(h * HALF, (h + 1) * HALF)
+            nc.tensor.matmul_mx(
+                out=acc[b][h][:],
+                lhsT=w_codes[b][:, z * P : (z + 1) * P].bitcast(FP8X4),
+                lhsT_scale=w_scales[b][:, z * P : (z + 1) * P],
+                rhs=x_codes[z][h][:].bitcast(FP8X4),
+                rhs_scale=x_scales[z][:, entries],
+                start=(z == 0),
+                stop=(z == 1),
+            )
 
-        gather_v(picked[0][:, 0, 0:START_V], plane[0][0], offs_sb, 0, START_V)
-        gather_s(picked[0][:, 0, START_V:S], plane[0][0], offs_sb, START_V, S)
-        gather_v(picked[0][:, 1, :], plane[0][1], offs_sb, 0, S)
-        gather_s(picked[0][:, 2, :], plane[0][2], offs_sb, 0, S)
-        gather_v(picked[0][:, 3, 0:HALF], plane[0][3], offs_sb, 0, HALF)
-        gather_s(picked[0][:, 3, HALF:S], plane[0][3], offs_sb, HALF, S)
-        weave(nc.vector.tensor_copy, 0, 0, WEAVE0_V)
-        weave(nc.scalar.copy, 0, WEAVE0_V, S)
-        gather_s(picked[1][:, 0, :], plane[1][0], offs_sb, 0, S)
-        quantize_x(0)
-        gather_v(picked[1][:, 1, :], plane[1][1], offs_sb, 0, S)
-        gather_v(picked[1][:, 2, 0:THIRD_V], plane[1][2], offs_sb, 0, THIRD_V)
-        gather_s(picked[1][:, 2, THIRD_V:S], plane[1][2], offs_sb, THIRD_V, S)
-        gather_v(picked[1][:, 3, 0:HALF], plane[1][3], offs_sb, 0, HALF)
-        gather_s(picked[1][:, 3, HALF:S], plane[1][3], offs_sb, HALF, S)
-        weave(nc.vector.tensor_copy, 1, 0, WEAVE_V)
-        weave(nc.scalar.copy, 1, WEAVE_V, S)
-        interleave_w(nc.vector.tensor_copy, 0, 0)
+        for z in range(2):
+            by_entry = grouped[z][:].rearrange("p (c j) -> p c j", j=4)
+            for j in range(4):
+                gather_v(by_entry[:, 0:HALF, j], plane[z][j], offs_sb, 0, HALF)
+                helped = HELP if (z, j) == (0, 0) else 0
+                if helped:
+                    gather_v(picked[z][:, j, 0:helped], plane[z][j], offs_sb, HALF, HALF + helped)
+                gather_s(picked[z][:, j, helped:], plane[z][j], offs_sb, HALF + helped, S)
+            cut = HALF + WEAVE_V[z]
+            interleave(nc.vector.tensor_copy, grouped[z][:, 4 * HALF : 4 * cut], picked[z][:, :, 0 : WEAVE_V[z]])
+            interleave(nc.scalar.copy, grouped[z][:, 4 * cut :], picked[z][:, :, WEAVE_V[z] :])
+            x_codes.append([
+                keep.tile([P, HALF], U32, name="x_codes%d0" % z, tag="x%d3" % z, align_bytes=64),
+                keep.tile([P, HALF], U32, name="x_codes%d1" % z, align_bytes=64),
+            ])
+            quantize_x(z, 0)
+            quantize_x(z, 1)
+        interleave_w(nc.scalar.copy, 0, 0)
         interleave_w(nc.scalar.copy, 1, 0)
-        quantize_x(1)
         quantize_w(0, 0, 1)
-        multiply(0, 0)
-        interleave_w(nc.scalar.copy, 0, 1)
-        interleave_w(nc.vector.tensor_copy, 1, 1)
+        multiply(0, 0, 0)
+        multiply(0, 0, 1)
+        interleave_w(nc.vector.tensor_copy, 0, 1)
+        interleave_w(nc.vector.tensor_copy, 1, 1, 0, P // 2)
+        interleave_w(nc.scalar.copy, 1, 1, P // 2, P)
         quantize_w(0, 1, 2)
-        multiply(0, 1)
-        w_codes.append(keep.tile([P, 2 * P], U32, name="w_codes1", tag="w_raw1", align_bytes=64))
+        multiply(0, 1, 0)
+        multiply(0, 1, 1)
         quantize_w(1, 0, 2)
         gather_s(old0[:, 0:FIRST], store[0][:], slot_sb, 0, FIRST)
-        gather_s(old0[:, FIRST:OLD_S], store[0][:], slot_sb, FIRST, OLD_S)
-        gather_v(old0[:, OLD_S:S], store[0][:], slot_sb, OLD_S, S)
-        multiply(1, 0)
-        multiply(1, 1)
+        gather_v(old0[:, FIRST : FIRST + OLD_V], store[0][:], slot_sb, FIRST, FIRST + OLD_V)
+        gather_s(old0[:, FIRST + OLD_V : S], store[0][:], slot_sb, FIRST + OLD_V, S)
+        for h in range(2):
+            multiply(1, 0, h)
+            multiply(1, 1, h)
         new0a = keep.tile([P, FIRST], F32, name="new0a")
         nc.vector.tensor_tensor(new0a[:], acc[0][0][:, 0:FIRST], old0[:, 0:FIRST], ADD)
         nc.scalar.activation(store[0][:].indirect(slot_sb[:, 0 : FIRST // 16]), new0a[:], COPY)

@@ -16,9 +16,10 @@ COPY = mybir.ActivationFunctionType.Copy
 
 P = 128
 HALF = S // 2
-GROUPS = [[(0, 1), (1, 3), (3, 4)], [(0, 2), (2, 3), (3, 4)]]
-HELP = 128
-WEAVE_V = [128, 160]
+GROUPS = [[(0, 2), (2, 4)], [(0, 2), (2, 3), (3, 4)]]
+WEAVE0_V = 352
+DIRECT = 224
+WEAVE1_V = 416
 FIRST = 128
 OLD_V = 224
 
@@ -34,7 +35,7 @@ def tile_picked_idxput_add_e_kernel(tc, xT, mem, w1, offs, slot, out):
 
         offs_sb = keep.tile([P, S // 16], U16, name="offs_sb")
         slot_sb = keep.tile([P, S // 16], U16, name="slot_sb")
-        loads = [[keep.tile([P, j1 - j0, T], F32, name="x%d%d" % (z, j0), tag="x%d%d" % (z, j0), align_bytes=64) for j0, j1 in GROUPS[z]] for z in range(2)]
+        loads = [[keep.tile([P, j1 - j0, T], F32, name="x%d%d" % (z, j0), align_bytes=64) for j0, j1 in GROUPS[z]] for z in range(2)]
         plane = [[loads[z][g][:, j - j0, :] for g, (j0, j1) in enumerate(GROUPS[z]) for j in range(j0, j1)] for z in range(2)]
         w_raw = [keep.tile([P, 4, N], F32, name="w_raw%d" % z, align_bytes=64) for z in range(2)]
         store = [keep.tile([P, U], F32, name="store%d" % b) for b in range(2)]
@@ -50,9 +51,10 @@ def tile_picked_idxput_add_e_kernel(tc, xT, mem, w1, offs, slot, out):
         for b in range(2):
             nc.sync.dma_start(out=store[b][:], in_=mem[b * P : (b + 1) * P, :])
 
-        picked = [keep.tile([P, 4, HALF], F32, name="picked%d" % z, align_bytes=64) for z in range(2)]
+        picked0 = keep.tile([P, 4, S], F32, name="picked0", align_bytes=64)
+        picked1 = keep.tile([P, 4, S - DIRECT], F32, name="picked1", align_bytes=64)
         grouped = [keep.tile([P, S * 4], BF16, name="grouped%d" % z, align_bytes=64) for z in range(2)]
-        x_codes = []
+        x_codes = [[keep.tile([P, HALF], U32, name="x_codes%d%d" % (z, h), align_bytes=64) for h in range(2)] for z in range(2)]
         x_scales = [keep.tile([P, S], U8, name="x_scales%d" % z, align_bytes=64) for z in range(2)]
         w_grouped = [keep.tile([P, 2 * 4 * P], BF16, name="w_grouped%d" % b, align_bytes=64) for b in range(2)]
         w_codes = [keep.tile([P, 2 * P], U32, name="w_codes%d" % b, align_bytes=64) for b in range(2)]
@@ -60,6 +62,11 @@ def tile_picked_idxput_add_e_kernel(tc, xT, mem, w1, offs, slot, out):
         acc = [[psum.tile([P, HALF], F32, name="acc%d%d" % (b, h)) for h in range(2)] for b in range(2)]
         old0 = keep.tile([P, S], F32, name="old0", tag="old0")
         old1 = keep.tile([P, S], F32, name="old1")
+
+        warm_in = keep.tile([P, 1], F32, name="warm_in")
+        warm_out = keep.tile([P, 1], F32, name="warm_out")
+        nc.vector.memset(warm_in[:], 0.0)
+        nc.scalar.activation(warm_out[:], warm_in[:], COPY)
 
         def gather_v(dst, window, lst, lo, hi):
             nc.vector.tensor_copy(dst, window.indirect(lst[:, lo // 16 : hi // 16]))
@@ -93,23 +100,26 @@ def tile_picked_idxput_add_e_kernel(tc, xT, mem, w1, offs, slot, out):
                 stop=(z == 1),
             )
 
-        for z in range(2):
-            by_entry = grouped[z][:].rearrange("p (c j) -> p c j", j=4)
-            for j in range(4):
-                gather_v(by_entry[:, 0:HALF, j], plane[z][j], offs_sb, 0, HALF)
-                helped = HELP if (z, j) == (0, 0) else 0
-                if helped:
-                    gather_v(picked[z][:, j, 0:helped], plane[z][j], offs_sb, HALF, HALF + helped)
-                gather_s(picked[z][:, j, helped:], plane[z][j], offs_sb, HALF + helped, S)
-            cut = HALF + WEAVE_V[z]
-            interleave(nc.vector.tensor_copy, grouped[z][:, 4 * HALF : 4 * cut], picked[z][:, :, 0 : WEAVE_V[z]])
-            interleave(nc.scalar.copy, grouped[z][:, 4 * cut :], picked[z][:, :, WEAVE_V[z] :])
-            x_codes.append([
-                keep.tile([P, HALF], U32, name="x_codes%d0" % z, tag="x%d3" % z, align_bytes=64),
-                keep.tile([P, HALF], U32, name="x_codes%d1" % z, align_bytes=64),
-            ])
-            quantize_x(z, 0)
-            quantize_x(z, 1)
+        def interleave_pair(copy, j0, lo, hi):
+            dst = grouped[0][:, 4 * lo : 4 * hi].rearrange("p (c i j) -> p c j i", i=4, j=4)[:, :, j0 : j0 + 2, :]
+            copy(out=dst, in_=picked0[:, j0 : j0 + 2, lo:hi].rearrange("p j (c i) -> p c j i", i=4))
+
+        for j0 in (0, 2):
+            gather_v(picked0[:, j0, :], plane[0][j0], offs_sb, 0, S)
+            gather_s(picked0[:, j0 + 1, :], plane[0][j0 + 1], offs_sb, 0, S)
+            interleave_pair(nc.vector.tensor_copy, j0, 0, HALF)
+            interleave_pair(nc.vector.tensor_copy, j0, HALF, WEAVE0_V)
+            interleave_pair(nc.scalar.copy, j0, WEAVE0_V, S)
+        quantize_x(0, 0)
+        quantize_x(0, 1)
+        by_entry = grouped[1][:].rearrange("p (c j) -> p c j", j=4)
+        for j in range(4):
+            gather_v(by_entry[:, 0:DIRECT, j], plane[1][j], offs_sb, 0, DIRECT)
+            gather_s(picked1[:, j, :], plane[1][j], offs_sb, DIRECT, S)
+        for copy, lo, hi in ((nc.vector.tensor_copy, DIRECT, HALF), (nc.vector.tensor_copy, HALF, WEAVE1_V), (nc.scalar.copy, WEAVE1_V, S)):
+            interleave(copy, grouped[1][:, 4 * lo : 4 * hi], picked1[:, :, lo - DIRECT : hi - DIRECT])
+        quantize_x(1, 0)
+        quantize_x(1, 1)
         interleave_w(nc.scalar.copy, 0, 0)
         interleave_w(nc.scalar.copy, 1, 0)
         quantize_w(0, 0, 1)

@@ -16,8 +16,9 @@ COPY = mybir.ActivationFunctionType.Copy
 
 P = 128
 HALF = S // 2
-GROUPS = [[(0, 2), (2, 4)], [(0, 2), (2, 3), (3, 4)]]
-WEAVE0_V = 352
+GROUPS = [[(0, 1), (1, 3), (3, 4)], [(0, 2), (2, 3), (3, 4)]]
+START_V = 384
+WEAVE0_S = 192
 DIRECT = 224
 WEAVE1_V = 416
 FIRST = 128
@@ -63,11 +64,6 @@ def tile_picked_idxput_add_e_kernel(tc, xT, mem, w1, offs, slot, out):
         old0 = keep.tile([P, S], F32, name="old0", tag="old0")
         old1 = keep.tile([P, S], F32, name="old1")
 
-        warm_in = keep.tile([P, 1], F32, name="warm_in")
-        warm_out = keep.tile([P, 1], F32, name="warm_out")
-        nc.vector.memset(warm_in[:], 0.0)
-        nc.scalar.activation(warm_out[:], warm_in[:], COPY)
-
         def gather_v(dst, window, lst, lo, hi):
             nc.vector.tensor_copy(dst, window.indirect(lst[:, lo // 16 : hi // 16]))
 
@@ -100,18 +96,16 @@ def tile_picked_idxput_add_e_kernel(tc, xT, mem, w1, offs, slot, out):
                 stop=(z == 1),
             )
 
-        def interleave_pair(copy, j0, lo, hi):
-            dst = grouped[0][:, 4 * lo : 4 * hi].rearrange("p (c i j) -> p c j i", i=4, j=4)[:, :, j0 : j0 + 2, :]
-            copy(out=dst, in_=picked0[:, j0 : j0 + 2, lo:hi].rearrange("p j (c i) -> p c j i", i=4))
-
-        for j0 in (0, 2):
-            gather_v(picked0[:, j0, :], plane[0][j0], offs_sb, 0, S)
-            gather_s(picked0[:, j0 + 1, :], plane[0][j0 + 1], offs_sb, 0, S)
-            interleave_pair(nc.vector.tensor_copy, j0, 0, HALF)
-            interleave_pair(nc.vector.tensor_copy, j0, HALF, WEAVE0_V)
-            interleave_pair(nc.scalar.copy, j0, WEAVE0_V, S)
-        quantize_x(0, 0)
+        gather_v(picked0[:, 0, 0:START_V], plane[0][0], offs_sb, 0, START_V)
+        gather_s(picked0[:, 0, START_V:S], plane[0][0], offs_sb, START_V, S)
+        gather_v(picked0[:, 1, :], plane[0][1], offs_sb, 0, S)
+        gather_s(picked0[:, 2, :], plane[0][2], offs_sb, 0, S)
+        gather_v(picked0[:, 3, 0:HALF], plane[0][3], offs_sb, 0, HALF)
+        gather_s(picked0[:, 3, HALF:S], plane[0][3], offs_sb, HALF, S)
+        for copy, lo, hi in ((nc.vector.tensor_copy, HALF, S), (nc.vector.tensor_copy, WEAVE0_S, HALF), (nc.scalar.copy, 0, WEAVE0_S)):
+            interleave(copy, grouped[0][:, 4 * lo : 4 * hi], picked0[:, :, lo:hi])
         quantize_x(0, 1)
+        quantize_x(0, 0)
         by_entry = grouped[1][:].rearrange("p (c j) -> p c j", j=4)
         for j in range(4):
             gather_v(by_entry[:, 0:DIRECT, j], plane[1][j], offs_sb, 0, DIRECT)

@@ -16,11 +16,9 @@ COPY = mybir.ActivationFunctionType.Copy
 
 P = 128
 HALF = S // 2
-GROUPS = [[(0, 1), (1, 3), (3, 4)], [(0, 2), (2, 3), (3, 4)]]
-START_V = 384
-WEAVE0_S = 192
+GROUPS = [(0, 2), (2, 3), (3, 4)]
 DIRECT = 224
-WEAVE1_V = 416
+WEAVE_V = [384, 416]
 FIRST = 128
 OLD_V = 224
 
@@ -36,13 +34,13 @@ def tile_picked_idxput_add_e_kernel(tc, xT, mem, w1, offs, slot, out):
 
         offs_sb = keep.tile([P, S // 16], U16, name="offs_sb")
         slot_sb = keep.tile([P, S // 16], U16, name="slot_sb")
-        loads = [[keep.tile([P, j1 - j0, T], F32, name="x%d%d" % (z, j0), align_bytes=64) for j0, j1 in GROUPS[z]] for z in range(2)]
-        plane = [[loads[z][g][:, j - j0, :] for g, (j0, j1) in enumerate(GROUPS[z]) for j in range(j0, j1)] for z in range(2)]
+        loads = [[keep.tile([P, j1 - j0, T], F32, name="x%d%d" % (z, j0), align_bytes=64) for j0, j1 in GROUPS] for z in range(2)]
+        plane = [[loads[z][g][:, j - j0, :] for g, (j0, j1) in enumerate(GROUPS) for j in range(j0, j1)] for z in range(2)]
         w_raw = [keep.tile([P, 4, N], F32, name="w_raw%d" % z, align_bytes=64) for z in range(2)]
         store = [keep.tile([P, U], F32, name="store%d" % b) for b in range(2)]
 
         for z in range(2):
-            for g, (j0, j1) in enumerate(GROUPS[z]):
+            for g, (j0, j1) in enumerate(GROUPS):
                 nc.sync.dma_start(out=loads[z][g][:], in_=x_rows[z][:, j0:j1, :])
                 if z == 0 and g == 0:
                     nc.sync.dma_start(offs_sb[:], offs)
@@ -52,8 +50,7 @@ def tile_picked_idxput_add_e_kernel(tc, xT, mem, w1, offs, slot, out):
         for b in range(2):
             nc.sync.dma_start(out=store[b][:], in_=mem[b * P : (b + 1) * P, :])
 
-        picked0 = keep.tile([P, 4, S], F32, name="picked0", align_bytes=64)
-        picked1 = keep.tile([P, 4, S - DIRECT], F32, name="picked1", align_bytes=64)
+        picked = [keep.tile([P, 4, S - DIRECT], F32, name="picked%d" % z, align_bytes=64) for z in range(2)]
         grouped = [keep.tile([P, S * 4], BF16, name="grouped%d" % z, align_bytes=64) for z in range(2)]
         x_codes = [[keep.tile([P, HALF], U32, name="x_codes%d%d" % (z, h), align_bytes=64) for h in range(2)] for z in range(2)]
         x_scales = [keep.tile([P, S], U8, name="x_scales%d" % z, align_bytes=64) for z in range(2)]
@@ -63,6 +60,11 @@ def tile_picked_idxput_add_e_kernel(tc, xT, mem, w1, offs, slot, out):
         acc = [[psum.tile([P, HALF], F32, name="acc%d%d" % (b, h)) for h in range(2)] for b in range(2)]
         old0 = keep.tile([P, S], F32, name="old0", tag="old0")
         old1 = keep.tile([P, S], F32, name="old1")
+
+        warm_in = keep.tile([P, 1], F32, name="warm_in")
+        warm_out = keep.tile([P, 1], F32, name="warm_out")
+        nc.vector.memset(warm_in[:], 0.0)
+        nc.scalar.activation(warm_out[:], warm_in[:], COPY)
 
         def gather_v(dst, window, lst, lo, hi):
             nc.vector.tensor_copy(dst, window.indirect(lst[:, lo // 16 : hi // 16]))
@@ -96,24 +98,15 @@ def tile_picked_idxput_add_e_kernel(tc, xT, mem, w1, offs, slot, out):
                 stop=(z == 1),
             )
 
-        gather_v(picked0[:, 0, 0:START_V], plane[0][0], offs_sb, 0, START_V)
-        gather_s(picked0[:, 0, START_V:S], plane[0][0], offs_sb, START_V, S)
-        gather_v(picked0[:, 1, :], plane[0][1], offs_sb, 0, S)
-        gather_s(picked0[:, 2, :], plane[0][2], offs_sb, 0, S)
-        gather_v(picked0[:, 3, 0:HALF], plane[0][3], offs_sb, 0, HALF)
-        gather_s(picked0[:, 3, HALF:S], plane[0][3], offs_sb, HALF, S)
-        for copy, lo, hi in ((nc.vector.tensor_copy, HALF, S), (nc.vector.tensor_copy, WEAVE0_S, HALF), (nc.scalar.copy, 0, WEAVE0_S)):
-            interleave(copy, grouped[0][:, 4 * lo : 4 * hi], picked0[:, :, lo:hi])
-        quantize_x(0, 1)
-        quantize_x(0, 0)
-        by_entry = grouped[1][:].rearrange("p (c j) -> p c j", j=4)
-        for j in range(4):
-            gather_v(by_entry[:, 0:DIRECT, j], plane[1][j], offs_sb, 0, DIRECT)
-            gather_s(picked1[:, j, :], plane[1][j], offs_sb, DIRECT, S)
-        for copy, lo, hi in ((nc.vector.tensor_copy, DIRECT, HALF), (nc.vector.tensor_copy, HALF, WEAVE1_V), (nc.scalar.copy, WEAVE1_V, S)):
-            interleave(copy, grouped[1][:, 4 * lo : 4 * hi], picked1[:, :, lo - DIRECT : hi - DIRECT])
-        quantize_x(1, 0)
-        quantize_x(1, 1)
+        for z in range(2):
+            by_entry = grouped[z][:].rearrange("p (c j) -> p c j", j=4)
+            for j in range(4):
+                gather_v(by_entry[:, 0:DIRECT, j], plane[z][j], offs_sb, 0, DIRECT)
+                gather_s(picked[z][:, j, :], plane[z][j], offs_sb, DIRECT, S)
+            for copy, lo, hi in ((nc.vector.tensor_copy, DIRECT, HALF), (nc.vector.tensor_copy, HALF, WEAVE_V[z]), (nc.scalar.copy, WEAVE_V[z], S)):
+                interleave(copy, grouped[z][:, 4 * lo : 4 * hi], picked[z][:, :, lo - DIRECT : hi - DIRECT])
+            quantize_x(z, 0)
+            quantize_x(z, 1)
         interleave_w(nc.scalar.copy, 0, 0)
         interleave_w(nc.scalar.copy, 1, 0)
         quantize_w(0, 0, 1)

@@ -18,7 +18,8 @@ P = 128
 HALF = S // 2
 GROUPS = [(0, 2), (2, 3), (3, 4)]
 DIRECT = 224
-WEAVE_V = [384, 416]
+WEAVE_V = [384, 448]
+W_V = [96, 96]
 FIRST = 128
 OLD_V = 224
 
@@ -112,9 +113,9 @@ def tile_picked_idxput_add_e_kernel(tc, xT, mem, w1, offs, slot, out):
         quantize_w(0, 0, 1)
         multiply(0, 0, 0)
         multiply(0, 0, 1)
-        interleave_w(nc.vector.tensor_copy, 0, 1)
-        interleave_w(nc.vector.tensor_copy, 1, 1, 0, P // 2)
-        interleave_w(nc.scalar.copy, 1, 1, P // 2, P)
+        for b in range(2):
+            interleave_w(nc.vector.tensor_copy, b, 1, 0, W_V[b])
+            interleave_w(nc.scalar.copy, b, 1, W_V[b], P)
         quantize_w(0, 1, 2)
         multiply(0, 1, 0)
         multiply(0, 1, 1)

@@ -53,12 +53,13 @@ def tile_picked_idxput_add_e_kernel(tc, xT, mem, w1, offs, slot, out):
 
         picked = [keep.tile([P, 4, S - DIRECT], F32, name="picked%d" % z, align_bytes=64) for z in range(2)]
         grouped = [keep.tile([P, S * 4], BF16, name="grouped%d" % z, align_bytes=64) for z in range(2)]
-        x_codes = [[keep.tile([P, HALF], U32, name="x_codes%d%d" % (z, h), align_bytes=64) for h in range(2)] for z in range(2)]
+        x_codes = [keep.tile([P, S], U32, name="x_codes%d" % z, align_bytes=64) for z in range(2)]
         x_scales = [keep.tile([P, S], U8, name="x_scales%d" % z, align_bytes=64) for z in range(2)]
         w_grouped = [keep.tile([P, 2 * 4 * P], BF16, name="w_grouped%d" % b, align_bytes=64) for b in range(2)]
         w_codes = [keep.tile([P, 2 * P], U32, name="w_codes%d" % b, align_bytes=64) for b in range(2)]
         w_scales = [keep.tile([P, 2 * P], U8, name="w_scales%d" % b, align_bytes=64) for b in range(2)]
-        acc = [[psum.tile([P, HALF], F32, name="acc%d%d" % (b, h)) for h in range(2)] for b in range(2)]
+        acc0 = [psum.tile([P, HALF], F32, name="acc0%d" % h) for h in range(2)]
+        acc1 = psum.tile([P, S], F32, name="acc1")
         old0 = keep.tile([P, S], F32, name="old0", tag="old0")
         old1 = keep.tile([P, S], F32, name="old1")
 
@@ -78,7 +79,7 @@ def tile_picked_idxput_add_e_kernel(tc, xT, mem, w1, offs, slot, out):
 
         def quantize_x(z, h):
             lo, hi = h * HALF, (h + 1) * HALF
-            nc.vector.quantize_mx(out=x_codes[z][h][:].bitcast(FP8X4), scales=x_scales[z][:, lo:hi], in_=grouped[z][:, 4 * lo : 4 * hi])
+            nc.vector.quantize_mx(out=x_codes[z][:, lo:hi].bitcast(FP8X4), scales=x_scales[z][:, lo:hi], in_=grouped[z][:, 4 * lo : 4 * hi])
 
         def interleave_w(copy, b, z, lo=0, hi=P):
             interleave(copy, w_grouped[b][:, 4 * (z * P + lo) : 4 * (z * P + hi)], w_raw[z][:, :, b * P + lo : b * P + hi])
@@ -87,13 +88,13 @@ def tile_picked_idxput_add_e_kernel(tc, xT, mem, w1, offs, slot, out):
             cols = slice(z0 * P, z1 * P)
             nc.vector.quantize_mx(out=w_codes[b][:, cols].bitcast(FP8X4), scales=w_scales[b][:, cols], in_=w_grouped[b][:, 4 * z0 * P : 4 * z1 * P])
 
-        def multiply(b, z, h):
-            entries = slice(h * HALF, (h + 1) * HALF)
+        def multiply(acc, b, z, lo, hi):
+            entries = slice(lo, hi)
             nc.tensor.matmul_mx(
-                out=acc[b][h][:],
+                out=acc[:],
                 lhsT=w_codes[b][:, z * P : (z + 1) * P].bitcast(FP8X4),
                 lhsT_scale=w_scales[b][:, z * P : (z + 1) * P],
-                rhs=x_codes[z][h][:].bitcast(FP8X4),
+                rhs=x_codes[z][:, entries].bitcast(FP8X4),
                 rhs_scale=x_scales[z][:, entries],
                 start=(z == 0),
                 stop=(z == 1),
@@ -111,31 +112,29 @@ def tile_picked_idxput_add_e_kernel(tc, xT, mem, w1, offs, slot, out):
         interleave_w(nc.scalar.copy, 0, 0)
         interleave_w(nc.scalar.copy, 1, 0)
         quantize_w(0, 0, 1)
-        multiply(0, 0, 0)
-        multiply(0, 0, 1)
+        for h in range(2):
+            multiply(acc0[h], 0, 0, h * HALF, (h + 1) * HALF)
         for b in range(2):
             interleave_w(nc.vector.tensor_copy, b, 1, 0, W_V[b])
             interleave_w(nc.scalar.copy, b, 1, W_V[b], P)
         quantize_w(0, 1, 2)
-        multiply(0, 1, 0)
-        multiply(0, 1, 1)
+        for h in range(2):
+            multiply(acc0[h], 0, 1, h * HALF, (h + 1) * HALF)
         quantize_w(1, 0, 2)
         gather_s(old0[:, 0:FIRST], store[0][:], slot_sb, 0, FIRST)
         gather_v(old0[:, FIRST : FIRST + OLD_V], store[0][:], slot_sb, FIRST, FIRST + OLD_V)
         gather_s(old0[:, FIRST + OLD_V : S], store[0][:], slot_sb, FIRST + OLD_V, S)
-        for h in range(2):
-            multiply(1, 0, h)
-            multiply(1, 1, h)
+        for z in range(2):
+            multiply(acc1, 1, z, 0, S)
         new0a = keep.tile([P, FIRST], F32, name="new0a")
-        nc.vector.tensor_tensor(new0a[:], acc[0][0][:, 0:FIRST], old0[:, 0:FIRST], ADD)
+        nc.vector.tensor_tensor(new0a[:], acc0[0][:, 0:FIRST], old0[:, 0:FIRST], ADD)
         nc.scalar.activation(store[0][:].indirect(slot_sb[:, 0 : FIRST // 16]), new0a[:], COPY)
         new0b = keep.tile([P, S - FIRST], F32, name="new0b")
-        nc.vector.tensor_tensor(new0b[:, 0 : HALF - FIRST], acc[0][0][:, FIRST:HALF], old0[:, FIRST:HALF], ADD)
-        nc.vector.tensor_tensor(new0b[:, HALF - FIRST : S - FIRST], acc[0][1][:], old0[:, HALF:S], ADD)
+        nc.vector.tensor_tensor(new0b[:, 0 : HALF - FIRST], acc0[0][:, FIRST:HALF], old0[:, FIRST:HALF], ADD)
+        nc.vector.tensor_tensor(new0b[:, HALF - FIRST : S - FIRST], acc0[1][:], old0[:, HALF:S], ADD)
         gather_v(old1[:], store[1][:], slot_sb, 0, S)
         y1 = keep.tile([P, S], F32, name="y1", tag="old0")
-        for h in range(2):
-            nc.scalar.copy(out=y1[:, h * HALF : (h + 1) * HALF], in_=acc[1][h][:])
+        nc.scalar.copy(out=y1[:], in_=acc1[:])
         nc.scalar.activation(store[0][:].indirect(slot_sb[:, FIRST // 16 : S // 16]), new0b[:], COPY)
         nc.sync.dma_start(out=out[0:P, :], in_=store[0][:])
         nc.vector.tensor_tensor(store[1][:].indirect(slot_sb[:]), old1[:], y1[:], ADD)

@@ -19,7 +19,7 @@ HALF = S // 2
 GROUPS = [(0, 2), (2, 3), (3, 4)]
 DIRECT = 224
 WEAVE_V = [384, 448]
-W_V = [96, 96]
+W_V = [96, 64]
 FIRST = 128
 OLD_V = 224
 

@@ -20,6 +20,7 @@ GROUPS = [(0, 2), (2, 3), (3, 4)]
 DIRECT = 224
 WEAVE_V = [384, 448]
 W_V = [96, 64]
+MEM1_PIECES = [(0, 512), (512, 768), (768, U)]
 FIRST = 128
 OLD_V = 224
 
@@ -48,8 +49,9 @@ def tile_picked_idxput_add_e_kernel(tc, xT, mem, w1, offs, slot, out):
         for z in range(2):
             nc.sync.dma_start(out=w_raw[z][:], in_=w_rows[z])
         nc.sync.dma_start(slot_sb[:], slot)
-        for b in range(2):
-            nc.sync.dma_start(out=store[b][:], in_=mem[b * P : (b + 1) * P, :])
+        nc.sync.dma_start(out=store[0][:], in_=mem[0:P, :])
+        for lo, hi in MEM1_PIECES:
+            nc.sync.dma_start(out=store[1][:, lo:hi], in_=mem[P:N, lo:hi])
 
         picked = [keep.tile([P, 4, S - DIRECT], F32, name="picked%d" % z, align_bytes=64) for z in range(2)]
         grouped = [keep.tile([P, S * 4], BF16, name="grouped%d" % z, align_bytes=64) for z in range(2)]

@@ -22,7 +22,7 @@ WEAVE_V = [384, 448]
 W_V = [96, 64]
 MEM1_PIECES = [(0, 512), (512, 768), (768, U)]
 FIRST = 128
-OLD_V = 224
+OLD_V = 256
 
 
 def tile_picked_idxput_add_e_kernel(tc, xT, mem, w1, offs, slot, out):

@@ -36,10 +36,10 @@ def tile_picked_idxput_add_e_kernel(tc, xT, mem, w1, offs, slot, out):
 
         offs_sb = keep.tile([P, S // 16], U16, name="offs_sb")
         slot_sb = keep.tile([P, S // 16], U16, name="slot_sb")
-        loads = [[keep.tile([P, j1 - j0, T], F32, name="x%d%d" % (z, j0), align_bytes=64) for j0, j1 in GROUPS] for z in range(2)]
+        loads = [[keep.tile([P, j1 - j0, T], F32, name="x%d%d" % (z, j0), align_bytes=256) for j0, j1 in GROUPS] for z in range(2)]
         plane = [[loads[z][g][:, j - j0, :] for g, (j0, j1) in enumerate(GROUPS) for j in range(j0, j1)] for z in range(2)]
-        w_raw = [keep.tile([P, 4, N], F32, name="w_raw%d" % z, align_bytes=64) for z in range(2)]
-        store = [keep.tile([P, U], F32, name="store%d" % b) for b in range(2)]
+        w_raw = [keep.tile([P, 4, N], F32, name="w_raw%d" % z, align_bytes=256) for z in range(2)]
+        store = [keep.tile([P, U], F32, name="store%d" % b, align_bytes=256) for b in range(2)]
 
         for z in range(2):
             for g, (j0, j1) in enumerate(GROUPS):

@@ -18,7 +18,7 @@ P = 128
 HALF = S // 2
 GROUPS = [(0, 2), (2, 3), (3, 4)]
 DIRECT = 224
-WEAVE_V = [384, 448]
+WEAVE_V = 448
 W_V = [96, 64]
 MEM1_PIECES = [(0, 512), (512, 768), (768, U)]
 FIRST = 128
@@ -36,16 +36,18 @@ def tile_picked_idxput_add_e_kernel(tc, xT, mem, w1, offs, slot, out):
 
         offs_sb = keep.tile([P, S // 16], U16, name="offs_sb")
         slot_sb = keep.tile([P, S // 16], U16, name="slot_sb")
-        loads = [[keep.tile([P, j1 - j0, T], F32, name="x%d%d" % (z, j0), align_bytes=256) for j0, j1 in GROUPS] for z in range(2)]
-        plane = [[loads[z][g][:, j - j0, :] for g, (j0, j1) in enumerate(GROUPS) for j in range(j0, j1)] for z in range(2)]
+        two = [keep.tile([P, 2 * T], F32, name="two%d" % e, align_bytes=256) for e in range(2)]
+        loads = [keep.tile([P, j1 - j0, T], F32, name="x1%d" % j0, align_bytes=256) for j0, j1 in GROUPS]
+        plane = [loads[g][:, j - j0, :] for g, (j0, j1) in enumerate(GROUPS) for j in range(j0, j1)]
         w_raw = [keep.tile([P, 4, N], F32, name="w_raw%d" % z, align_bytes=256) for z in range(2)]
         store = [keep.tile([P, U], F32, name="store%d" % b, align_bytes=256) for b in range(2)]
 
-        for z in range(2):
-            for g, (j0, j1) in enumerate(GROUPS):
-                nc.sync.dma_start(out=loads[z][g][:], in_=x_rows[z][:, j0:j1, :])
-                if z == 0 and g == 0:
-                    nc.sync.dma_start(offs_sb[:], offs)
+        for e in range(2):
+            nc.sync.dma_start(out=two[e][:], in_=x_rows[0][:, 2 * e : 2 * e + 2, :].rearrange("p j t -> p (j t)"))
+            if e == 0:
+                nc.sync.dma_start(offs_sb[:], offs)
+        for g, (j0, j1) in enumerate(GROUPS):
+            nc.sync.dma_start(out=loads[g][:], in_=x_rows[1][:, j0:j1, :])
         for z in range(2):
             nc.sync.dma_start(out=w_raw[z][:], in_=w_rows[z])
         nc.sync.dma_start(slot_sb[:], slot)
@@ -53,7 +55,7 @@ def tile_picked_idxput_add_e_kernel(tc, xT, mem, w1, offs, slot, out):
         for lo, hi in MEM1_PIECES:
             nc.sync.dma_start(out=store[1][:, lo:hi], in_=mem[P:N, lo:hi])
 
-        picked = [keep.tile([P, 4, S - DIRECT], F32, name="picked%d" % z, align_bytes=64) for z in range(2)]
+        picked = keep.tile([P, 4, S - DIRECT], F32, name="picked", align_bytes=64)
         grouped = [keep.tile([P, S * 4], BF16, name="grouped%d" % z, align_bytes=64) for z in range(2)]
         x_codes = [keep.tile([P, S], U32, name="x_codes%d" % z, align_bytes=64) for z in range(2)]
         x_scales = [keep.tile([P, S], U8, name="x_scales%d" % z, align_bytes=64) for z in range(2)]
@@ -84,7 +86,12 @@ def tile_picked_idxput_add_e_kernel(tc, xT, mem, w1, offs, slot, out):
             nc.vector.quantize_mx(out=x_codes[z][:, lo:hi].bitcast(FP8X4), scales=x_scales[z][:, lo:hi], in_=grouped[z][:, 4 * lo : 4 * hi])
 
         def interleave_w(copy, b, z, lo=0, hi=P):
-            interleave(copy, w_grouped[b][:, 4 * (z * P + lo) : 4 * (z * P + hi)], w_raw[z][:, :, b * P + lo : b * P + hi])
+            dst = w_grouped[b][:, 4 * (z * P + lo) : 4 * (z * P + hi)]
+            src = w_raw[z][:, :, b * P + lo : b * P + hi]
+            if z == 0:
+                copy(out=dst.rearrange("p (c i u e) -> p c e u i", i=4, u=2, e=2), in_=src.rearrange("p (e u) (c i) -> p c e u i", e=2, i=4))
+            else:
+                interleave(copy, dst, src)
 
         def quantize_w(b, z0, z1):
             cols = slice(z0 * P, z1 * P)
@@ -102,15 +109,21 @@ def tile_picked_idxput_add_e_kernel(tc, xT, mem, w1, offs, slot, out):
                 stop=(z == 1),
             )
 
-        for z in range(2):
-            by_entry = grouped[z][:].rearrange("p (c j) -> p c j", j=4)
-            for j in range(4):
-                gather_v(by_entry[:, 0:DIRECT, j], plane[z][j], offs_sb, 0, DIRECT)
-                gather_s(picked[z][:, j, :], plane[z][j], offs_sb, DIRECT, S)
-            for copy, lo, hi in ((nc.vector.tensor_copy, DIRECT, HALF), (nc.vector.tensor_copy, HALF, WEAVE_V[z]), (nc.scalar.copy, WEAVE_V[z], S)):
-                interleave(copy, grouped[z][:, 4 * lo : 4 * hi], picked[z][:, :, lo - DIRECT : hi - DIRECT])
-            quantize_x(z, 0)
-            quantize_x(z, 1)
+        by_entry = grouped[0][:].rearrange("p (c j) -> p c j", j=4)
+        for e, ranges in enumerate((((0, S),), ((0, HALF), (HALF, S)))):
+            for lo, hi in ranges:
+                gather_s(by_entry[:, lo:hi, e], two[e][:], offs_sb, lo, hi)
+                gather_v(by_entry[:, lo:hi, 2 + e], two[e][:, T : 2 * T], offs_sb, lo, hi)
+        quantize_x(0, 0)
+        quantize_x(0, 1)
+        by_entry = grouped[1][:].rearrange("p (c j) -> p c j", j=4)
+        for j in range(4):
+            gather_v(by_entry[:, 0:DIRECT, j], plane[j], offs_sb, 0, DIRECT)
+            gather_s(picked[:, j, :], plane[j], offs_sb, DIRECT, S)
+        for copy, lo, hi in ((nc.vector.tensor_copy, DIRECT, HALF), (nc.vector.tensor_copy, HALF, WEAVE_V), (nc.scalar.copy, WEAVE_V, S)):
+            interleave(copy, grouped[1][:, 4 * lo : 4 * hi], picked[:, :, lo - DIRECT : hi - DIRECT])
+        quantize_x(1, 0)
+        quantize_x(1, 1)
         interleave_w(nc.scalar.copy, 0, 0)
         interleave_w(nc.scalar.copy, 1, 0)
         quantize_w(0, 0, 1)

@@ -20,7 +20,7 @@ GROUPS = [(0, 2), (2, 3), (3, 4)]
 DIRECT = 224
 WEAVE_V = 448
 W_V = [96, 64]
-MEM1_PIECES = [(0, 512), (512, 768), (768, U)]
+MEM1_PIECES = [(0, 512), (512, 768), (768, 896), (896, U)]
 FIRST = 128
 OLD_V = 256
 

@@ -19,8 +19,9 @@ HALF = S // 2
 GROUPS = [(0, 2), (2, 3), (3, 4)]
 DIRECT = 224
 WEAVE_V = 448
+PASS0_PIECES = ((0, 256), (256, 384), (384, S))
 W_V = [96, 64]
-MEM1_PIECES = [(0, 512), (512, 768), (768, 896), (896, U)]
+MEM1_PIECES = [(0, 512), (512, 768), (768, U)]
 FIRST = 128
 OLD_V = 256
 
@@ -81,8 +82,7 @@ def tile_picked_idxput_add_e_kernel(tc, xT, mem, w1, offs, slot, out):
         def interleave(copy, dst, src):
             copy(out=dst.rearrange("p (c i j) -> p c j i", i=4, j=4), in_=src.rearrange("p j (c i) -> p c j i", i=4))
 
-        def quantize_x(z, h):
-            lo, hi = h * HALF, (h + 1) * HALF
+        def quantize_x(z, lo, hi):
             nc.vector.quantize_mx(out=x_codes[z][:, lo:hi].bitcast(FP8X4), scales=x_scales[z][:, lo:hi], in_=grouped[z][:, 4 * lo : 4 * hi])
 
         def interleave_w(copy, b, z, lo=0, hi=P):
@@ -110,20 +110,21 @@ def tile_picked_idxput_add_e_kernel(tc, xT, mem, w1, offs, slot, out):
             )
 
         by_entry = grouped[0][:].rearrange("p (c j) -> p c j", j=4)
-        for e, ranges in enumerate((((0, S),), ((0, HALF), (HALF, S)))):
-            for lo, hi in ranges:
+        for e, (ranges_s, ranges_v) in enumerate(((((0, S),), ((0, S),)), (PASS0_PIECES, ((0, HALF), (HALF, S))))):
+            for lo, hi in ranges_s:
                 gather_s(by_entry[:, lo:hi, e], two[e][:], offs_sb, lo, hi)
+            for lo, hi in ranges_v:
                 gather_v(by_entry[:, lo:hi, 2 + e], two[e][:, T : 2 * T], offs_sb, lo, hi)
-        quantize_x(0, 0)
-        quantize_x(0, 1)
+        for lo, hi in PASS0_PIECES:
+            quantize_x(0, lo, hi)
         by_entry = grouped[1][:].rearrange("p (c j) -> p c j", j=4)
         for j in range(4):
             gather_v(by_entry[:, 0:DIRECT, j], plane[j], offs_sb, 0, DIRECT)
             gather_s(picked[:, j, :], plane[j], offs_sb, DIRECT, S)
         for copy, lo, hi in ((nc.vector.tensor_copy, DIRECT, HALF), (nc.vector.tensor_copy, HALF, WEAVE_V), (nc.scalar.copy, WEAVE_V, S)):
             interleave(copy, grouped[1][:, 4 * lo : 4 * hi], picked[:, :, lo - DIRECT : hi - DIRECT])
-        quantize_x(1, 0)
-        quantize_x(1, 1)
+        quantize_x(1, 0, HALF)
+        quantize_x(1, HALF, S)
         interleave_w(nc.scalar.copy, 0, 0)
         interleave_w(nc.scalar.copy, 1, 0)
         quantize_w(0, 0, 1)
@@ -151,6 +152,7 @@ def tile_picked_idxput_add_e_kernel(tc, xT, mem, w1, offs, slot, out):
         y1 = keep.tile([P, S], F32, name="y1", tag="old0")
         nc.scalar.copy(out=y1[:], in_=acc1[:])
         nc.scalar.activation(store[0][:].indirect(slot_sb[:, FIRST // 16 : S // 16]), new0b[:], COPY)
-        nc.sync.dma_start(out=out[0:P, :], in_=store[0][:])
+        for lo, hi in ((0, U // 2), (U // 2, U)):
+            nc.sync.dma_start(out=out[0:P, lo:hi], in_=store[0][:, lo:hi])
         nc.vector.tensor_tensor(store[1][:].indirect(slot_sb[:]), old1[:], y1[:], ADD)
         nc.sync.dma_start(out=out[P:N, :], in_=store[1][:])

@@ -16,10 +16,9 @@ COPY = mybir.ActivationFunctionType.Copy
 
 P = 128
 HALF = S // 2
-GROUPS = [(0, 2), (2, 3), (3, 4)]
-DIRECT = 224
-WEAVE_V = 448
 PASS0_PIECES = ((0, 256), (256, 384), (384, S))
+PLAIN_S = 64
+PLAIN_V = 320
 W_V = [96, 64]
 MEM1_PIECES = [(0, 512), (512, 768), (768, U)]
 FIRST = 128
@@ -37,18 +36,17 @@ def tile_picked_idxput_add_e_kernel(tc, xT, mem, w1, offs, slot, out):
 
         offs_sb = keep.tile([P, S // 16], U16, name="offs_sb")
         slot_sb = keep.tile([P, S // 16], U16, name="slot_sb")
-        two = [keep.tile([P, 2 * T], F32, name="two%d" % e, align_bytes=256) for e in range(2)]
-        loads = [keep.tile([P, j1 - j0, T], F32, name="x1%d" % j0, align_bytes=256) for j0, j1 in GROUPS]
-        plane = [loads[g][:, j - j0, :] for g, (j0, j1) in enumerate(GROUPS) for j in range(j0, j1)]
+        two = [keep.tile([P, 2 * T], F32, name="two%d" % i, align_bytes=256) for i in range(3)]
+        one = [keep.tile([P, T], F32, name="one%d" % i, align_bytes=256) for i in range(2)]
         w_raw = [keep.tile([P, 4, N], F32, name="w_raw%d" % z, align_bytes=256) for z in range(2)]
         store = [keep.tile([P, U], F32, name="store%d" % b, align_bytes=256) for b in range(2)]
 
-        for e in range(2):
-            nc.sync.dma_start(out=two[e][:], in_=x_rows[0][:, 2 * e : 2 * e + 2, :].rearrange("p j t -> p (j t)"))
-            if e == 0:
+        for i in range(3):
+            nc.sync.dma_start(out=two[i][:], in_=x_rows[i // 2][:, 2 * (i % 2) : 2 * (i % 2) + 2, :].rearrange("p j t -> p (j t)"))
+            if i == 0:
                 nc.sync.dma_start(offs_sb[:], offs)
-        for g, (j0, j1) in enumerate(GROUPS):
-            nc.sync.dma_start(out=loads[g][:], in_=x_rows[1][:, j0:j1, :])
+        for i in range(2):
+            nc.sync.dma_start(out=one[i][:], in_=x_rows[1][:, 2 + i, :])
         for z in range(2):
             nc.sync.dma_start(out=w_raw[z][:], in_=w_rows[z])
         nc.sync.dma_start(slot_sb[:], slot)
@@ -56,7 +54,8 @@ def tile_picked_idxput_add_e_kernel(tc, xT, mem, w1, offs, slot, out):
         for lo, hi in MEM1_PIECES:
             nc.sync.dma_start(out=store[1][:, lo:hi], in_=mem[P:N, lo:hi])
 
-        picked = keep.tile([P, 4, S - DIRECT], F32, name="picked", align_bytes=64)
+        plain_s = keep.tile([P, 4, PLAIN_S], F32, name="plain_s", align_bytes=64)
+        plain_v = keep.tile([P, 4, S - PLAIN_V], F32, name="plain_v", align_bytes=64)
         grouped = [keep.tile([P, S * 4], BF16, name="grouped%d" % z, align_bytes=64) for z in range(2)]
         x_codes = [keep.tile([P, S], U32, name="x_codes%d" % z, align_bytes=64) for z in range(2)]
         x_scales = [keep.tile([P, S], U8, name="x_scales%d" % z, align_bytes=64) for z in range(2)]
@@ -79,19 +78,13 @@ def tile_picked_idxput_add_e_kernel(tc, xT, mem, w1, offs, slot, out):
         def gather_s(dst, window, lst, lo, hi):
             nc.scalar.activation(dst, window.indirect(lst[:, lo // 16 : hi // 16]), COPY)
 
-        def interleave(copy, dst, src):
-            copy(out=dst.rearrange("p (c i j) -> p c j i", i=4, j=4), in_=src.rearrange("p j (c i) -> p c j i", i=4))
-
         def quantize_x(z, lo, hi):
             nc.vector.quantize_mx(out=x_codes[z][:, lo:hi].bitcast(FP8X4), scales=x_scales[z][:, lo:hi], in_=grouped[z][:, 4 * lo : 4 * hi])
 
         def interleave_w(copy, b, z, lo=0, hi=P):
             dst = w_grouped[b][:, 4 * (z * P + lo) : 4 * (z * P + hi)]
             src = w_raw[z][:, :, b * P + lo : b * P + hi]
-            if z == 0:
-                copy(out=dst.rearrange("p (c i u e) -> p c e u i", i=4, u=2, e=2), in_=src.rearrange("p (e u) (c i) -> p c e u i", e=2, i=4))
-            else:
-                interleave(copy, dst, src)
+            copy(out=dst.rearrange("p (c i u e) -> p c e u i", i=4, u=2, e=2), in_=src.rearrange("p (e u) (c i) -> p c e u i", e=2, i=4))
 
         def quantize_w(b, z0, z1):
             cols = slice(z0 * P, z1 * P)
@@ -118,11 +111,20 @@ def tile_picked_idxput_add_e_kernel(tc, xT, mem, w1, offs, slot, out):
         for lo, hi in PASS0_PIECES:
             quantize_x(0, lo, hi)
         by_entry = grouped[1][:].rearrange("p (c j) -> p c j", j=4)
-        for j in range(4):
-            gather_v(by_entry[:, 0:DIRECT, j], plane[j], offs_sb, 0, DIRECT)
-            gather_s(picked[:, j, :], plane[j], offs_sb, DIRECT, S)
-        for copy, lo, hi in ((nc.vector.tensor_copy, DIRECT, HALF), (nc.vector.tensor_copy, HALF, WEAVE_V), (nc.scalar.copy, WEAVE_V, S)):
-            interleave(copy, grouped[1][:, 4 * lo : 4 * hi], picked[:, :, lo - DIRECT : hi - DIRECT])
+        direct = by_entry[:, PLAIN_S:PLAIN_V, :]
+        gather_s(direct[:, :, 0], two[2][:], offs_sb, PLAIN_S, PLAIN_V)
+        gather_v(direct[:, :, 2], two[2][:, T : 2 * T], offs_sb, PLAIN_S, PLAIN_V)
+        for e in range(2):
+            gather_s(plain_s[:, 2 * e, :], two[2][:, e * T : (e + 1) * T], offs_sb, 0, PLAIN_S)
+            gather_v(plain_v[:, 2 * e, :], two[2][:, e * T : (e + 1) * T], offs_sb, PLAIN_V, S)
+        gather_s(direct[:, :, 1], one[0][:], offs_sb, PLAIN_S, PLAIN_V)
+        gather_s(plain_s[:, 1, :], one[0][:], offs_sb, 0, PLAIN_S)
+        gather_v(plain_v[:, 1, :], one[0][:], offs_sb, PLAIN_V, S)
+        gather_v(direct[:, :, 3], one[1][:], offs_sb, PLAIN_S, PLAIN_V)
+        gather_s(plain_s[:, 3, :], one[1][:], offs_sb, 0, PLAIN_S)
+        gather_s(plain_v[:, 3, :], one[1][:], offs_sb, PLAIN_V, S)
+        for copy, plain, lo, hi in ((nc.vector.tensor_copy, plain_v, PLAIN_V, S), (nc.scalar.copy, plain_s, 0, PLAIN_S)):
+            copy(out=grouped[1][:, 4 * lo : 4 * hi].rearrange("p (c i j) -> p c j i", i=4, j=4), in_=plain[:].rearrange("p j (c i) -> p c j i", i=4))
         quantize_x(1, 0, HALF)
         quantize_x(1, HALF, S)
         interleave_w(nc.scalar.copy, 0, 0)

from contextlib import ExitStack

import concourse.mybir as mybir

K, T, S, N, U = 1024, 1024, 512, 256, 1024
FLOPS = 2 * K * N * S

F32 = mybir.dt.float32
BF16 = mybir.dt.bfloat16
U32 = mybir.dt.uint32
U16 = mybir.dt.uint16
U8 = mybir.dt.uint8
FP8X4 = mybir.dt.float8_e4m3fn_x4
ADD = mybir.AluOpType.add
COPY = mybir.ActivationFunctionType.Copy

P = 128
HALF = S // 2
PASS0_PIECES = ((0, 256), (256, 384), (384, S))
PLAIN_S = 64
PLAIN_V = 320
W_V = [96, 64]
MEM1_PIECES = [(0, 512), (512, 768), (768, U)]
FIRST = 128
OLD_V = 256


def tile_picked_idxput_add_e_kernel(tc, xT, mem, w1, offs, slot, out):
    nc = tc.nc
    with ExitStack() as ctx:
        keep = ctx.enter_context(tc.tile_pool(name="keep", bufs=1))
        psum = ctx.enter_context(tc.psum_pool(name="psum", bufs=1))

        x_rows = xT.rearrange("(z p j) t -> z p j t", z=2, p=P, j=4)
        w_rows = w1.rearrange("(z p j) m -> z p j m", z=2, p=P, j=4)

        offs_sb = keep.tile([P, S // 16], U16, name="offs_sb")
        slot_sb = keep.tile([P, S // 16], U16, name="slot_sb")
        two = [keep.tile([P, 2 * T], F32, name="two%d" % i, align_bytes=256) for i in range(3)]
        one = [keep.tile([P, T], F32, name="one%d" % i, align_bytes=256) for i in range(2)]
        w_raw = [keep.tile([P, 4, N], F32, name="w_raw%d" % z, align_bytes=256) for z in range(2)]
        store = [keep.tile([P, U], F32, name="store%d" % b, align_bytes=256) for b in range(2)]

        for i in range(3):
            nc.sync.dma_start(out=two[i][:], in_=x_rows[i // 2][:, 2 * (i % 2) : 2 * (i % 2) + 2, :].rearrange("p j t -> p (j t)"))
            if i == 0:
                nc.sync.dma_start(offs_sb[:], offs)
        for i in range(2):
            nc.sync.dma_start(out=one[i][:], in_=x_rows[1][:, 2 + i, :])
        for z in range(2):
            nc.sync.dma_start(out=w_raw[z][:], in_=w_rows[z])
        nc.sync.dma_start(slot_sb[:], slot)
        nc.sync.dma_start(out=store[0][:], in_=mem[0:P, :])
        for lo, hi in MEM1_PIECES:
            nc.sync.dma_start(out=store[1][:, lo:hi], in_=mem[P:N, lo:hi])

        plain_s = keep.tile([P, 4, PLAIN_S], F32, name="plain_s", align_bytes=64)
        plain_v = keep.tile([P, 4, S - PLAIN_V], F32, name="plain_v", align_bytes=64)
        grouped = [keep.tile([P, S * 4], BF16, name="grouped%d" % z, align_bytes=64) for z in range(2)]
        x_codes = [keep.tile([P, S], U32, name="x_codes%d" % z, align_bytes=64) for z in range(2)]
        x_scales = [keep.tile([P, S], U8, name="x_scales%d" % z, align_bytes=64) for z in range(2)]
        w_grouped = [keep.tile([P, 2 * 4 * P], BF16, name="w_grouped%d" % b, align_bytes=64) for b in range(2)]
        w_codes = [keep.tile([P, 2 * P], U32, name="w_codes%d" % b, align_bytes=64) for b in range(2)]
        w_scales = [keep.tile([P, 2 * P], U8, name="w_scales%d" % b, align_bytes=64) for b in range(2)]
        acc0 = [psum.tile([P, HALF], F32, name="acc0%d" % h) for h in range(2)]
        acc1 = psum.tile([P, S], F32, name="acc1")
        old0 = keep.tile([P, S], F32, name="old0", tag="old0")
        old1 = keep.tile([P, S], F32, name="old1")

        warm_in = keep.tile([P, 1], F32, name="warm_in")
        warm_out = keep.tile([P, 1], F32, name="warm_out")
        nc.vector.memset(warm_in[:], 0.0)
        nc.scalar.activation(warm_out[:], warm_in[:], COPY)

        def gather_v(dst, window, lst, lo, hi):
            nc.vector.tensor_copy(dst, window.indirect(lst[:, lo // 16 : hi // 16]))

        def gather_s(dst, window, lst, lo, hi):
            nc.scalar.activation(dst, window.indirect(lst[:, lo // 16 : hi // 16]), COPY)

        def quantize_x(z, lo, hi):
            nc.vector.quantize_mx(out=x_codes[z][:, lo:hi].bitcast(FP8X4), scales=x_scales[z][:, lo:hi], in_=grouped[z][:, 4 * lo : 4 * hi])

        def interleave_w(copy, b, z, lo=0, hi=P):
            dst = w_grouped[b][:, 4 * (z * P + lo) : 4 * (z * P + hi)]
            src = w_raw[z][:, :, b * P + lo : b * P + hi]
            copy(out=dst.rearrange("p (c i u e) -> p c e u i", i=4, u=2, e=2), in_=src.rearrange("p (e u) (c i) -> p c e u i", e=2, i=4))

        def quantize_w(b, z0, z1):
            cols = slice(z0 * P, z1 * P)
            nc.vector.quantize_mx(out=w_codes[b][:, cols].bitcast(FP8X4), scales=w_scales[b][:, cols], in_=w_grouped[b][:, 4 * z0 * P : 4 * z1 * P])

        def multiply(acc, b, z, lo, hi):
            entries = slice(lo, hi)
            nc.tensor.matmul_mx(
                out=acc[:],
                lhsT=w_codes[b][:, z * P : (z + 1) * P].bitcast(FP8X4),
                lhsT_scale=w_scales[b][:, z * P : (z + 1) * P],
                rhs=x_codes[z][:, entries].bitcast(FP8X4),
                rhs_scale=x_scales[z][:, entries],
                start=(z == 0),
                stop=(z == 1),
            )

        by_entry = grouped[0][:].rearrange("p (c j) -> p c j", j=4)
        for e, (ranges_s, ranges_v) in enumerate(((((0, S),), ((0, S),)), (PASS0_PIECES, ((0, HALF), (HALF, S))))):
            for lo, hi in ranges_s:
                gather_s(by_entry[:, lo:hi, e], two[e][:], offs_sb, lo, hi)
            for lo, hi in ranges_v:
                gather_v(by_entry[:, lo:hi, 2 + e], two[e][:, T : 2 * T], offs_sb, lo, hi)
        for lo, hi in PASS0_PIECES:
            quantize_x(0, lo, hi)
        by_entry = grouped[1][:].rearrange("p (c j) -> p c j", j=4)
        direct = by_entry[:, PLAIN_S:PLAIN_V, :]
        gather_s(direct[:, :, 0], two[2][:], offs_sb, PLAIN_S, PLAIN_V)
        gather_v(direct[:, :, 2], two[2][:, T : 2 * T], offs_sb, PLAIN_S, PLAIN_V)
        for e in range(2):
            gather_s(plain_s[:, 2 * e, :], two[2][:, e * T : (e + 1) * T], offs_sb, 0, PLAIN_S)
            gather_v(plain_v[:, 2 * e, :], two[2][:, e * T : (e + 1) * T], offs_sb, PLAIN_V, S)
        gather_s(direct[:, :, 1], one[0][:], offs_sb, PLAIN_S, PLAIN_V)
        gather_s(plain_s[:, 1, :], one[0][:], offs_sb, 0, PLAIN_S)
        gather_v(plain_v[:, 1, :], one[0][:], offs_sb, PLAIN_V, S)
        gather_v(direct[:, :, 3], one[1][:], offs_sb, PLAIN_S, PLAIN_V)
        gather_s(plain_s[:, 3, :], one[1][:], offs_sb, 0, PLAIN_S)
        gather_s(plain_v[:, 3, :], one[1][:], offs_sb, PLAIN_V, S)
        for copy, plain, lo, hi in ((nc.vector.tensor_copy, plain_v, PLAIN_V, S), (nc.scalar.copy, plain_s, 0, PLAIN_S)):
            copy(out=grouped[1][:, 4 * lo : 4 * hi].rearrange("p (c i j) -> p c j i", i=4, j=4), in_=plain[:].rearrange("p j (c i) -> p c j i", i=4))
        quantize_x(1, 0, HALF)
        quantize_x(1, HALF, S)
        interleave_w(nc.scalar.copy, 0, 0)
        interleave_w(nc.scalar.copy, 1, 0)
        quantize_w(0, 0, 1)
        for h in range(2):
            multiply(acc0[h], 0, 0, h * HALF, (h + 1) * HALF)
        for b in range(2):
            interleave_w(nc.vector.tensor_copy, b, 1, 0, W_V[b])
            interleave_w(nc.scalar.copy, b, 1, W_V[b], P)
        quantize_w(0, 1, 2)
        for h in range(2):
            multiply(acc0[h], 0, 1, h * HALF, (h + 1) * HALF)
        quantize_w(1, 0, 2)
        gather_s(old0[:, 0:FIRST], store[0][:], slot_sb, 0, FIRST)
        gather_v(old0[:, FIRST : FIRST + OLD_V], store[0][:], slot_sb, FIRST, FIRST + OLD_V)
        gather_s(old0[:, FIRST + OLD_V : S], store[0][:], slot_sb, FIRST + OLD_V, S)
        for z in range(2):
            multiply(acc1, 1, z, 0, S)
        new0a = keep.tile([P, FIRST], F32, name="new0a")
        nc.vector.tensor_tensor(new0a[:], acc0[0][:, 0:FIRST], old0[:, 0:FIRST], ADD)
        nc.scalar.activation(store[0][:].indirect(slot_sb[:, 0 : FIRST // 16]), new0a[:], COPY)
        new0b = keep.tile([P, S - FIRST], F32, name="new0b")
        nc.vector.tensor_tensor(new0b[:, 0 : HALF - FIRST], acc0[0][:, FIRST:HALF], old0[:, FIRST:HALF], ADD)
        nc.vector.tensor_tensor(new0b[:, HALF - FIRST : S - FIRST], acc0[1][:], old0[:, HALF:S], ADD)
        gather_v(old1[:], store[1][:], slot_sb, 0, S)
        y1 = keep.tile([P, S], F32, name="y1", tag="old0")
        nc.scalar.copy(out=y1[:], in_=acc1[:])
        nc.scalar.activation(store[0][:].indirect(slot_sb[:, FIRST // 16 : S // 16]), new0b[:], COPY)
        for lo, hi in ((0, U // 2), (U // 2, U)):
            nc.sync.dma_start(out=out[0:P, lo:hi], in_=store[0][:, lo:hi])
        nc.vector.tensor_tensor(store[1][:].indirect(slot_sb[:]), old1[:], y1[:], ADD)
        nc.sync.dma_start(out=out[P:N, :], in_=store[1][:])
